import numpy as np, ml_dtypes
CORES = [9,25,41,57]
N = 4
BF = ml_dtypes.bfloat16
def gentries(a):
    return np.ascontiguousarray(a.reshape(8, 16, -1).transpose(0, 2, 1)).reshape(8, -1)
def gtable(e):
    e = np.asarray(e); return np.ascontiguousarray(e.reshape(8, -1, 16).transpose(0, 2, 1)).reshape(128, -1).astype(np.int32)
P, A, M, Q = 65536, 4, 8, 512
S = N * P
def letters(rng, w, n):
    a = np.add.accumulate(w); return np.searchsorted(a[:-1], rng.random(n) * a[-1], side="right")
def places(rng):
    p = rng.integers(0, S + 1, (N, 8, 2, Q)); u = P // 8
    v = rng.integers(0, 8 * N + 1, p.shape) * u + rng.integers(-1, 2, p.shape)
    p = np.sort(np.where(rng.random(p.shape) < 0.25, np.minimum(np.maximum(v, 0), S), p), axis=2)
    k = (8 * np.arange(N)[:, None] + np.arange(8)) * u
    p[:, :, 0, Q - 5] = k; p[:, :, 1, Q - 5] = k + u; p[:, :, :, Q - 4] = S; p[:, :, :, Q - 3] = 0
    p[:, :, 1, Q - 2] = p[:, :, 0, Q - 2]; p[:, :, 0, Q - 1] = 0; p[:, :, 1, Q - 1] = S
    return p
def pack(s, e, p):
    return {"bwt": np.ascontiguousarray(np.asarray(s).reshape(8, N, P).transpose(1, 0, 2)).astype(np.int32), "pats": np.stack([gtable(e[r].reshape(8, M * Q)) for r in range(N)]), "starts": np.stack([gtable(p[r].reshape(8, 2 * Q)) for r in range(N)])}
def bw(t):
    n = len(t); key = np.zeros(n, np.int64); k = 62 // (A - 1).bit_length()
    for i in range(k): key = key * A + np.roll(t, -i)
    while True:
        o = np.argsort(key); ks = key[o]
        v = np.zeros(n, np.int64); v[o[1:]] = np.add.accumulate((ks[1:] != ks[:-1]).astype(np.int64))
        if v.max() == n - 1 or k >= n: break
        key = (v * n + np.roll(v, -k)) * n + np.roll(v, -2 * k); k *= 3
    return t[o - 1]
def setup_inputs(rng):
    s = []; e = rng.integers(0, A, (N, 8, M, Q)); h = Q // 2
    for g in range(8):
        w = np.exp2(rng.integers(0, 4, A)); c = rng.integers(0, A); w[c] += 4 * A
        s.append(np.concatenate([letters(rng, w * np.exp2(rng.integers(0, 3, A)), P) for r in range(N)]))
        e[:, g, :, :h] = np.where(rng.random((N, M, h)) < 0.875, c, e[:, g, :, :h])
    return pack(np.stack(s), e, places(rng))
def setup_inputs_ends(rng):
    i = np.arange(S); s = np.zeros((8, S), np.int64)
    s[0] = i * A // S; s[1] = A - 1 - s[0]; s[2] = i % A; s[3] = rng.integers(0, A - 1, S); s[4] = rng.integers(1, A, S); s[5] = i // P % A
    s[6] = np.where((i % P == 0) | (i % P == P - 1), A - 1, rng.integers(0, A - 1, S)); s[7] = np.where(i == S - 1, A - 1, rng.integers(0, A - 1, S))
    e = rng.integers(0, A, (N, 8, M, Q)); e[..., 0] = 0; e[..., 1] = A - 1; e[..., 2] = 0; e[:, :, 0, 2] = A - 1; e[..., 3] = 0; e[:, :, M - 1, 3] = A - 1
    q = rng.integers(0, N); e[q] = rng.integers(0, A, (8, M, 1)); e[q, 0] = e[q, 0, 0, 0]
    p = places(rng); p[:, :, 0, :4] = 0; p[:, :, 1, :4] = S; p[q, :, 0] = 0; p[q, :, 1] = S
    return pack(s, e, p)
def setup_inputs_one(rng):
    k = (np.arange(8) + rng.integers(0, A)) % A; c = k[None, :, None, None]
    e = np.where(rng.random((N, 8, 1, Q)) < 0.5, c, rng.integers(0, A, (N, 8, M, Q))); e[..., 0] = k[None, :, None]
    return pack(np.repeat(k[:, None], S, axis=1), e, places(rng))
def setup_inputs_text(rng):
    s = []; e = np.zeros((N, 8, M, Q), np.int64); h = Q // 2
    for g in range(8):
        t = np.tile(letters(rng, np.exp2(rng.integers(0, 3, A)), S // 8), 8); t = np.where(rng.random(S) < 0.03125, rng.integers(0, A, S), t); s.append(bw(t))
        e[:, g] = t[(rng.integers(0, S, (N, 1, Q)) + (M - 1 - np.arange(M))[None, :, None]) % S]
    e[..., h:] = np.where(rng.random((N, 8, M, Q - h)) < 0.0625, rng.integers(0, A, (N, 8, M, Q - h)), e[..., h:])
    p = places(rng); p[:, :, 0, :h] = 0; p[:, :, 1, :h] = S
    return pack(np.stack(s), e, p)
def setup_inputs_spread(rng):
    s = np.stack([np.concatenate([letters(rng, np.exp2(-2.0 * rng.permutation(A)), P) for r in range(N)]) for g in range(8)])
    e = np.stack([s[g][rng.integers(0, S, (N, M, Q))] for g in range(8)], axis=1)
    p = places(rng); p[:, :, 1] = np.minimum(p[:, :, 0] + (rng.integers(0, S + 1, (N, 8, Q)) >> rng.integers(0, 20, (N, 8, Q))), S)
    return pack(s, np.where(rng.random((N, 8, 1, Q)) < 0.5, e, rng.integers(0, A, (N, 8, M, Q))), p)
def check_inputs(d):
    bad = [k + " out of range" for k in ("bwt", "pats") if not ((d[k] >= 0) & (d[k] < A)).all()]
    if not ((d["starts"] >= 0) & (d["starts"] <= S)).all(): bad.append("starts out of range")
    p = np.stack([gentries(a) for a in d["starts"]]).reshape(N, 8, 2, Q)
    if (p[:, :, 0] > p[:, :, 1]).any(): bad.append("lo over hi in starts")
    return bad
def reference(bwt, pats, starts):
    s = bwt.transpose(1, 0, 2).reshape(8, S)
    e = np.stack([gentries(pats[r]) for r in range(N)]).reshape(N, 8, M, Q)
    b = np.stack([gentries(starts[r]) for r in range(N)]).reshape(N, 8, 2, Q).astype(np.int64)
    ends = np.zeros((N, 8, 2, Q), np.int64)
    for g in range(8):
        C = np.array([np.count_nonzero(s[g] < c) for c in range(A)]); occ = np.zeros((A, S + 1), np.int64)
        for c in range(A): occ[c, 1:] = np.add.accumulate((s[g] == c).astype(np.int64))
        p = b[:, g]
        for t in range(M):
            c = e[:, g, t][:, None]; p = C[c] + occ[c, p]
        ends[:, g] = p
    return {"y": np.asarray(np.stack([gtable(ends[r].reshape(8, 2 * Q)) for r in range(N)]), np.float32)}

@@ -1,0 +1,300 @@
+import math
+import numpy as np
+from concourse.bass import DstId, RemoteDMATransfer
+from concourse.mybir import AluOpType as A, ActivationFunctionType as F
+
+NR, PC, ST, QN = 4, 65536, 8, 512
+KC = 30718 - 2040
+SCRATCH = {
+    "X": ("sbuf", [128, 4096], "int32"), "Xb": ("sbuf", [128, 4096], "bfloat16"), "Xe": ("sbuf", [128, 4096], "bfloat16"),
+    "V": ("sbuf", [128, 16384], "int32"), "W": ("sbuf", [128, 4104], "float32"),
+    "wd": ("sbuf", [128, 512], "uint16"), "wi": ("sbuf", [128, 2048], "int32"),
+    "hi": ("sbuf", [128, 256], "int32"), "ni": ("sbuf", [128, 1024], "int32"), "nf": ("sbuf", [128, 1024], "float32"),
+    "sc": ("sbuf", [128, 1032], "float32"), "su": ("sbuf", [128, 1032], "uint16"), "zz": ("sbuf", [128, 256], "float32"),
+    "rt": ("sbuf", [128, 16], "float32"), "inc": ("sbuf", [128, 16], "float32"), "exc": ("sbuf", [128, 16], "float32"),
+    "bs": ("sbuf", [128, 264], "float32"), "bi": ("sbuf", [128, 264], "int32"),
+    "dg": ("sbuf", [128, 792], "int32"), "df": ("sbuf", [128, 792], "float16"), "M1": ("sbuf", [128, 264], "float32"),
+    "M0": ("sbuf", [128, 64], "bfloat16"), "km": ("sbuf", [128, 264], "float32"), "jq": ("sbuf", [128, 264], "int32"),
+    "xi": ("sbuf", [128, 264], "int32"), "xf": ("sbuf", [128, 144], "float32"), "pi": ("sbuf", [128, 1], "int32"),
+    "pk": ("sbuf", [128, 8], "int32"), "pf": ("sbuf", [128, 8], "float32"), "tc": ("sbuf", [128, 32], "float32"),
+    "E0": ("sbuf", [128, 144], "bfloat16"), "E1": ("sbuf", [128, 144], "bfloat16"), "ES": ("sbuf", [128, 144], "float16"),
+    "Id": ("sbuf", [128, 128], "bfloat16"), "xg": ("sbuf", [128, 128], "int32"), "BO": ("sbuf", [128, 128], "float32"),
+    "Lt": ("sbuf", [128, 16], "float32"), "m0i": ("sbuf", [128, 128], "int32"), "m0f": ("sbuf", [128, 128], "float32"),
+    "pats_s": ("sbuf", [128, 256], "int32"), "st_s": ("sbuf", [128, 64], "int32"), "cl": ("sbuf", [128, 256], "float32"),
+    "cz": ("sbuf", [128, 32], "int32"), "st4": ("sbuf", [128, 64], "int32"),
+    "psw": ("psum", [128, 512], "float32"), "psh": ("psum", [128, 512], "float32"), "psm": ("psum", [128, 512], "float32"),
+    "psd": ("psum", [128, 512], "float32"),
+}
+for _k in range(NR):
+    SCRATCH["vl%d" % _k] = ("sbuf", [128, 512], "uint16")
+    SCRATCH["wl%d" % _k] = ("sbuf", [128, 1032], "uint16")
+for _k in range(6):
+    SCRATCH["dm%d" % _k] = ("sbuf", [128, 128], "float16")
+for _h in range(2):
+    SCRATCH["ps%d" % _h] = ("psum", [128, 512], "float32")
+    SCRATCH["z%d" % _h] = ("sbuf", [128, 32], "int32")
+    SCRATCH["la%d" % _h] = ("sbuf", [128, 64], "int32")
+    SCRATCH["lb%d" % _h] = ("sbuf", [128, 96], "int32")
+    SCRATCH["ua%d" % _h] = ("sbuf", [128, 64], "uint16")
+    SCRATCH["ub%d" % _h] = ("sbuf", [128, 64], "uint16")
+    SCRATCH["r0%d" % _h] = ("sbuf", [128, 512], "bfloat16")
+    SCRATCH["r1%d" % _h] = ("sbuf", [128, 512], "float32")
+    SCRATCH["ya%d" % _h] = ("sbuf", [128, 512], "float16")
+    SCRATCH["yb%d" % _h] = ("sbuf", [128, 512], "float16")
+    SCRATCH["yo%d" % _h] = ("sbuf", [128, 32], "float32")
+SEMAPHORES = ["sv", "sa", "st", "sg", "ls", "ld0", "ld1", "ldp", "yd0", "yd1"] + ["v%d" % k for k in range(NR)] + ["w%d" % k for k in range(NR)]
+
+
+def rank_program(g, core, T, topo):
+    rank = T.rank_of(core)
+    if rank is None:
+        return
+    peers = [T.cores[(rank + d) % NR] for d in range(1, NR)]
+    S = T.sem
+    cnt, seen = {"sv": 0, "sa": 0, "st": 0, "sg": 0}, {}
+
+    def waits(q, name, deps):
+        for s, n in deps:
+            if seen.get((name, s), 0) < n:
+                q.wait_ge(S[s], n)
+                seen[(name, s)] = n
+
+    def op(q, name, call, args, deps, kw=None):
+        waits(q, name, deps)
+        call(*args, **(kw or {})).then_inc(S[name], 1)
+        cnt[name] += 1
+        return (name, cnt[name])
+
+    vec, act, ten, syn = g.vector, g.scalar, g.tensor, g.sync
+
+    def copy(out, in_, *deps):
+        return op(vec, "sv", vec.tensor_copy, (out, in_), deps)
+
+    def tt(out, a, b, o, *deps):
+        return op(vec, "sv", vec.tensor_tensor, (out, a, b, o), deps)
+
+    def ts(out, a, s1, o1, s2, o2, *deps):
+        if o2 is None:
+            return op(vec, "sv", vec.tensor_scalar, (out, a, s1, None, o1), deps)
+        return op(vec, "sv", vec.tensor_scalar, (out, a, s1, s2, o1, o2), deps)
+
+    def fill(ap, v, *deps):
+        return op(vec, "sv", vec.memset, (ap, v), deps)
+
+    def activ(out, in_, f, deps, **kw):
+        return op(act, "sa", act.activation, (out, in_, f), deps, kw)
+
+    def mms(items, deps):
+        waits(ten, "st", deps)
+        for i, (out, l, r, a, b) in enumerate(items):
+            m = ten.matmul(out, l, r, a, b)
+            if i == len(items) - 1:
+                m.then_inc(S.st, 1)
+        cnt["st"] += 1
+        return ("st", cnt["st"])
+
+    for j in range(2):
+        for w in range(16):
+            q = syn if w % 2 == 0 else act
+            q.dma_start(T.X[w::16, 2048 * j:2048 * (j + 1)], T.bwt[:, 4096 * w + 2048 * j:4096 * w + 2048 * (j + 1)]).then_inc(S["ld%d" % j], 16)
+    syn.dma_start(T.pats_s[:], T.pats[:]).then_inc(S.ldp, 16)
+    syn.dma_start(T.st_s[:], T.starts[:]).then_inc(S.ldp, 16)
+
+    g.iota(T.xi[:], [[1, 264]], 0, 0).then_inc(S.sg, 1)
+    g.iota(T.pi[:], [[1, 1]], 0, 1).then_inc(S.sg, 1)
+    G = ("sg", 2)
+    pk, pf, tc = T.pk, T.pf, T.tc
+
+    def k1(b, i):
+        return b[:, i:i + 1]
+    d = []
+    for i, (sh, mk) in enumerate([(0, 1), (1, 1), (2, 1), (3, 1), (0, 15), (0, 112), (0, 127)]):
+        d.append(ts(k1(pk, i), T.pi[:], sh, A.logical_shift_right, mk, A.bitwise_and, G))
+    dx = copy(T.xf[:], T.xi[:, 0:144], G)
+    dp = copy(pf[:, 0:7], pk[:, 0:7], d[-1])
+    ts(k1(tc, 0), k1(pf, 1), 3.0, A.mult, 1.0, A.add, dp)
+    ts(k1(tc, 1), k1(pf, 2), 15.0, A.mult, 1.0, A.add, dp)
+    t2 = ts(k1(tc, 2), k1(pf, 3), 255.0, A.mult, 1.0, A.add, dp)
+    d15 = ts(k1(tc, 3), k1(pf, 5), 15.0, A.add, None, None, dp)
+    t3 = tt(k1(tc, 4), k1(tc, 0), k1(tc, 1), A.mult, t2)
+    t4 = tt(k1(tc, 5), k1(tc, 4), k1(tc, 2), A.mult, t3)
+    t5 = tt(k1(tc, 6), k1(tc, 5), k1(pf, 0), A.mult, t4)
+    t6 = tt(k1(tc, 7), k1(tc, 5), k1(tc, 6), A.subtract, t5)
+    ts(T.E1[:], T.xf[:], k1(tc, 3), A.is_equal, k1(tc, 6), A.mult, t6)
+    dE = ts(T.E0[:], T.xf[:], k1(tc, 3), A.is_equal, k1(tc, 7), A.mult, t6)
+    dE = ts(T.Id[:], T.xf[:, 0:128], k1(pf, 6), A.is_equal, None, None, dx)
+    fill(T.zz[:], 0.0)
+    fill(T.W[:, 4096:4104], -2040.0)
+    dS0 = fill(T.sc[:], 0.0)
+
+    cb, ce, pkd, hd = [], [], None, None
+    NP = 4
+    pw = 4096 // NP
+    na = pw // 16
+
+    def rest_of_constants():
+        ts(T.ES[:], T.xf[:], k1(tc, 3), A.is_equal, 4.0, A.mult, dx)
+        a = ts(T.xg[:], T.xi[:, 0:128], 112, A.bitwise_and, None, None)
+        ts(T.BO[:], T.xg[:], k1(pf, 5), A.is_equal, None, None, a)
+        ts(T.Lt[:], T.xf[:, 0:16], k1(pf, 4), A.is_gt, None, None)
+        ts(T.m0i[:, 0:64], T.xi[:, 0:64], 2, A.logical_shift_right, None, None)
+        a = ts(T.m0i[:, 64:128], T.xi[:, 0:64], 3, A.bitwise_and, None, None)
+        ts(T.m0f[:, 0:64], T.m0i[:, 0:64], k1(pf, 4), A.is_gt, None, None, a)
+        a = ts(T.m0f[:, 64:128], T.m0i[:, 64:128], 1.0, A.add, None, None, a)
+        a = tt(T.m0f[:, 0:64], T.m0f[:, 0:64], T.m0f[:, 64:128], A.mult, a)
+        ts(T.M0[:], T.m0f[:, 0:64], -1.0, A.add, None, None, a)
+        a = ts(T.jq[:], T.xi[:], 15, A.bitwise_and, None, None)
+        ts(T.km[:], T.jq[:], k1(pf, 4), A.is_equal, -6144.0, A.mult, a)
+        ts(k1(tc, 8), k1(pf, 3), -448.0, A.mult, 448.0, A.add)
+        for i, v in enumerate([9, 8]):
+            ts(k1(tc, 10 + i), k1(pf, 4), float(v), A.is_equal, 256.0, A.mult)
+        for i, v in enumerate([11, 10, 13, 12]):
+            ts(k1(tc, 12 + i), k1(pf, 4), float(v), A.is_equal, None, None)
+        for i, v in enumerate([13, 12]):
+            a = ts(k1(tc, 16 + i), k1(pf, 4), float(v), A.is_equal, -2.0, A.mult)
+        b = tt(k1(tc, 18), k1(tc, 8), k1(pf, 0), A.mult, a)
+        b = tt(k1(tc, 19), k1(tc, 8), k1(tc, 18), A.subtract, b)
+        b = tt(tc[:, 20:22], tc[:, 18:20], tc[:, 10:12], A.add, b)
+        for par in range(2):
+            for i, col in enumerate([20, 12, 14]):
+                ts(T["dm%d" % (2 * i + par)][:], T.xf[:, 0:128], k1(pf, 6), A.is_equal, k1(tc, col + par), A.mult, b)
+            end = 257 if par == 0 else 256
+            b2 = ts(T.km[:, par:end:2], T.km[:, par:end:2], k1(tc, 16 + par), A.add, 2048.0, A.add, b)
+        waits(vec, "sv", [("ldp", 32)])
+        ts(T.cl[:], T.pats_s[:], 1048577.0, A.mult, -4.0 * KC, A.add)
+        ts(T.st4[:], T.st_s[:], 4.0, A.mult, None, None)
+        return ts(T.cz[:], T.pats_s[:, 0:32], 1048577.0, A.mult, None, None)
+
+    for j in range(NP):
+        sl = slice(pw * j, pw * (j + 1))
+        c = copy(T.Xb[:, sl], T.X[:, sl], ("ld%d" % (j * 2 // NP), 256))
+        e = activ(T.Xe[:, sl], T.Xb[:, sl], F.Exp, [c], scale=math.log(32.0))
+        items = []
+        for h, E in enumerate((T.E0, T.E1)):
+            for q in range(16):
+                items.append((T.psw[:, 256 * h + na * j:256 * h + na * (j + 1)], E[:, 15 - q:143 - q], T.Xb[:, pw * j + q:pw * (j + 1):16], q == 0, q == 15))
+        pkd = mms(items, [dE, c])
+        items = [(T.psh[:, na * j:na * (j + 1)], T.Id[:], T.Xe[:, pw * j + q:pw * (j + 1):16], q == 0, q == 15) for q in range(16)]
+        hd = mms(items, [e])
+    dK = rest_of_constants()
+
+    def send(buf, land, sem, deps):
+        waits(g, "gq", deps)
+        ids = [DstId(rid=topo.addr(p)[0], pnc=topo.addr(p)[1]) for p in peers]
+        g.remote_dma_fused([RemoteDMATransfer(dst_ids=ids, dma_engine_mask=topo.mask(core, peers[0]), remote_sem=S[sem], srcs=[buf[:]], dsts=[T[land][:] for _ in peers])], local_sem=S.ls)
+
+    ne = len(topo.engines(core, peers[0]))
+    cw = copy(T.wd[:], T.psw[:], pkd)
+    send(T.wd, "vl%d" % rank, "v%d" % rank, [cw])
+    own = copy(T.wi[:, 512 * rank:512 * rank + 512], T.psw[:])
+
+    def lists_a(h, src):
+        z, la, ua, lb, ub = T["z%d" % h], T["la%d" % h], T["ua%d" % h], T["lb%d" % h], T["ub%d" % h]
+        ts(la[:, 0:32], z[:], 63, A.bitwise_and, None, None, src)
+        a = ts(la[:, 32:64], z[:], 14, A.logical_shift_right, None, None, src)
+        ts(lb[:, 0:32], z[:], 6, A.logical_shift_right, 16383, A.bitwise_and)
+        ts(lb[:, 32:64], z[:], 6, A.logical_shift_right, 255, A.bitwise_and)
+        b = ts(lb[:, 64:96], z[:], 10, A.logical_shift_right, 0x1F00, A.bitwise_and)
+        ra = copy(ua[:], la[:], a)
+        b = tt(lb[:, 32:64], lb[:, 32:64], lb[:, 64:96], A.add, b)
+        rb = copy(ub[:], lb[:, 0:64], b)
+        return ra, rb
+
+    def masks(h, ra, dep1):
+        m0 = activ(T["r0%d" % h][:], T.M0[:].indirect(T["ua%d" % h][:, 0:32]), F.Copy, [ra])
+        m1 = activ(T["r1%d" % h][:], T.M1[:, 0:257].indirect(T["ua%d" % h][:, 32:64]), F.Copy, [ra] + dep1)
+        return m0, m1
+
+    a = copy(T.hi[:], T.psh[:, 0:256], hd)
+    for c in range(4):
+        b = ts(T.ni[:, 256 * c:256 * c + 256], T.hi[:], 5 * c, A.logical_shift_right, 31, A.bitwise_and, a)
+    b = copy(T.nf[:], T.ni[:], b)
+    for c in range(4):
+        s = op(vec, "sv", vec.tensor_tensor_scan, (T.sc[:, 258 * c + 1:258 * c + 257], T.nf[:, 256 * c:256 * c + 256], T.zz[:], 0.0, A.add, A.add), (b, dS0))
+    cs = copy(T.su[:], T.sc[:], s)
+    send(T.su, "wl%d" % rank, "w%d" % rank, [cs])
+
+    def unpack(r, dep):
+        x = None
+        for k in range(8):
+            x = ts(T.V[:, 4096 * r + 512 * k:4096 * r + 512 * k + 512], T.wi[:, 512 * r:512 * r + 512], 2 * k, A.logical_shift_right, 3, A.bitwise_and, dep)
+        return x
+
+    def counts(r, src):
+        for c in range(4):
+            ts(T.W[:, 1024 * c + 256 * r:1024 * c + 256 * r + 256], src[:, 258 * c:258 * c + 256], -2040.0, A.add, None, None)
+        return copy(T.rt[:, r::4], src[:, 256::258])
+
+    counts(rank, T.sc)
+    unpack(rank, own)
+    zr = []
+    for h in range(2):
+        zr.append(tt(T["z%d" % h][:], T.st4[:, 32 * h:32 * h + 32], T.cz[:], A.add, dK))
+    la = [lists_a(h, zr[h]) for h in range(2)]
+    order = [(rank + NR - dd) % NR for dd in range(1, NR)]
+    for r in order:
+        x = copy(T.wi[:, 512 * r:512 * r + 512], T["vl%d" % r][:], ("v%d" % r, ne))
+        dV = unpack(r, x)
+    for r in order:
+        waits(vec, "sv", [("w%d" % r, ne)])
+        dR = counts(r, T["wl%d" % r])
+    a = op(vec, "sv", vec.tensor_tensor_scan, (T.inc[:], T.rt[:], T.zz[:, 0:16], 0.0, A.add, A.add), (dR,))
+    copy(T.bs[:, 256:257], T.inc[:, 15:16], a)
+    a = tt(T.exc[:], T.inc[:], T.rt[:], A.subtract, a)
+    bd = []
+    for k in range(16):
+        o, s1, s2 = T.bs[:, 16 * k:16 * k + 16], T.rt[:, k:k + 1], T.exc[:, k:k + 1]
+        if k % 3 == 2:
+            bd.append(activ(o, T.Lt[:], F.Identity, [a], bias=s2, scale=s1))
+        else:
+            bd.append(ts(o, T.Lt[:], s1, A.mult, s2, A.add, a))
+    m = mms([(T.psm[:, 0:257], T.BO[:], T.bs[:, 0:257], True, True)], [bd[-1], bd[-2]])
+    a = copy(T.bi[:, 0:257], T.psm[:, 0:257], m)
+    ts(T.dg[:, 0:257], T.bi[:, 0:257], 11, A.logical_shift_right, None, None, a)
+    ts(T.dg[:, 257:514], T.bi[:, 0:257], 2046, A.bitwise_and, None, None, a)
+    a = ts(T.dg[:, 514:771], T.bi[:, 0:257], 1, A.bitwise_and, None, None, a)
+    a = copy(T.df[:, 0:771], T.dg[:, 0:771], a)
+    for par in range(2):
+        n = 129 - par
+        m = mms([(T.psd[:, 256 * par:256 * par + n], T["dm%d" % (2 * i + par)][:], T.df[:, 257 * i + par:257 * i + 257:2], i == 0, i == 2) for i in range(3)], [a])
+    for par in range(2):
+        n, end = 129 - par, 257 if par == 0 else 256
+        dM = tt(T.M1[:, par:end:2], T.psd[:, 256 * par:256 * par + n], T.km[:, par:end:2], A.add, m)
+
+    mk = [masks(h, la[h][0], [dM]) for h in range(2)]
+    lb = [la[0][1], la[1][1]]
+    res = [None, None]
+
+    def sums(h, y, first, dep):
+        items = [(T["ps%d" % h][:, 0:32], T.ES[:, 15 - q:143 - q], T[y][:, q::16], first and q == 0, (not first) and q == 15) for q in range(16)]
+        return mms(items, [dep])
+
+    def y1(h):
+        d = tt(T["ya%d" % h][:], T.V[:].indirect(T["ub%d" % h][:, 0:32]), T["r0%d" % h][:], A.is_equal, lb[h], mk[h][0])
+        sums(h, "ya%d" % h, True, d)
+
+    def y2(h):
+        d = tt(T["yb%d" % h][:], T.W[:, 0:4097].indirect(T["ub%d" % h][:, 32:64]), T["r1%d" % h][:], A.max, lb[h], mk[h][1])
+        res[h] = sums(h, "yb%d" % h, False, d)
+
+    def nxt(h, t):
+        z = tt(T["z%d" % h][:], T["ps%d" % h][:, 0:32], T.cl[:, 32 * t:32 * t + 32], A.add, res[h])
+        ra, rb = lists_a(h, z)
+        lb[h] = rb
+        mk[h] = masks(h, ra, [])
+
+    for t in range(ST):
+        y1(0)
+        if t:
+            nxt(1, t)
+        y2(0)
+        y1(1)
+        if t + 1 < ST:
+            nxt(0, t + 1)
+        y2(1)
+    for h in range(2):
+        d = ts(T["yo%d" % h][:], T["ps%d" % h][:, 0:32], 0.25, A.mult, -float(KC), A.add, res[h])
+        waits(syn, "sy", [d])
+        syn.dma_start(T.y[:, 32 * h:32 * h + 32], T["yo%d" % h][:]).then_inc(S["yd%d" % h], 16)
+    waits(syn, "sy", [("yd0", 16), ("yd1", 16)])
+    g.wait_ge(S.ls, 2 * ne)

@@ -3,14 +3,14 @@ import numpy as np
 from concourse.bass import DstId, RemoteDMATransfer
 from concourse.mybir import AluOpType as A, ActivationFunctionType as F
 
-NR, PC, ST, QN = 4, 65536, 8, 512
-KC = 30718 - 2040
+NR, ST = 4, 8
+KC = 30718 - 2048
 SCRATCH = {
     "X": ("sbuf", [128, 4096], "int32"), "Xb": ("sbuf", [128, 4096], "bfloat16"), "Xe": ("sbuf", [128, 4096], "bfloat16"),
     "V": ("sbuf", [128, 16384], "int32"), "W": ("sbuf", [128, 4104], "float32"),
-    "wd": ("sbuf", [128, 512], "uint16"), "wi": ("sbuf", [128, 2048], "int32"),
+    "wi": ("sbuf", [128, 2048], "int32"),
     "hi": ("sbuf", [128, 256], "int32"), "ni": ("sbuf", [128, 1024], "int32"), "nf": ("sbuf", [128, 1024], "float32"),
-    "sc": ("sbuf", [128, 1032], "float32"), "su": ("sbuf", [128, 1032], "uint16"), "zz": ("sbuf", [128, 256], "float32"),
+    "zz": ("sbuf", [128, 256], "float32"),
     "rt": ("sbuf", [128, 16], "float32"), "inc": ("sbuf", [128, 16], "float32"), "exc": ("sbuf", [128, 16], "float32"),
     "bs": ("sbuf", [128, 264], "float32"), "bi": ("sbuf", [128, 264], "int32"),
     "dg": ("sbuf", [128, 792], "int32"), "df": ("sbuf", [128, 792], "float16"), "M1": ("sbuf", [128, 264], "float32"),
@@ -18,16 +18,17 @@ SCRATCH = {
     "xi": ("sbuf", [128, 264], "int32"), "xf": ("sbuf", [128, 144], "float32"), "pi": ("sbuf", [128, 1], "int32"),
     "pk": ("sbuf", [128, 8], "int32"), "pf": ("sbuf", [128, 8], "float32"), "tc": ("sbuf", [128, 32], "float32"),
     "E0": ("sbuf", [128, 144], "bfloat16"), "E1": ("sbuf", [128, 144], "bfloat16"), "ES": ("sbuf", [128, 144], "float16"),
-    "Id": ("sbuf", [128, 128], "bfloat16"), "xg": ("sbuf", [128, 128], "int32"), "BO": ("sbuf", [128, 128], "float32"),
+    "Id": ("sbuf", [128, 128], "bfloat16"), "Ih": ("sbuf", [128, 128], "float16"),
+    "xg": ("sbuf", [128, 128], "int32"), "BO": ("sbuf", [128, 128], "float32"),
     "Lt": ("sbuf", [128, 16], "float32"), "m0i": ("sbuf", [128, 128], "int32"), "m0f": ("sbuf", [128, 128], "float32"),
     "pats_s": ("sbuf", [128, 256], "int32"), "st_s": ("sbuf", [128, 64], "int32"), "cl": ("sbuf", [128, 256], "float32"),
     "cz": ("sbuf", [128, 32], "int32"), "st4": ("sbuf", [128, 64], "int32"),
     "psw": ("psum", [128, 512], "float32"), "psh": ("psum", [128, 512], "float32"), "psm": ("psum", [128, 512], "float32"),
-    "psd": ("psum", [128, 512], "float32"),
+    "psd": ("psum", [128, 512], "float32"), "pa": ("psum", [128, 512], "float32"), "pb": ("psum", [128, 512], "float32"),
 }
 for _k in range(NR):
     SCRATCH["vl%d" % _k] = ("sbuf", [128, 512], "uint16")
-    SCRATCH["wl%d" % _k] = ("sbuf", [128, 1032], "uint16")
+    SCRATCH["wl%d" % _k] = ("sbuf", [128, 1028], "float16")
 for _k in range(6):
     SCRATCH["dm%d" % _k] = ("sbuf", [128, 128], "float16")
 for _h in range(2):
@@ -100,40 +101,34 @@ def rank_program(g, core, T, topo):
     syn.dma_start(T.pats_s[:], T.pats[:]).then_inc(S.ldp, 16)
     syn.dma_start(T.st_s[:], T.starts[:]).then_inc(S.ldp, 16)
 
-    g.iota(T.xi[:], [[1, 264]], 0, 0).then_inc(S.sg, 1)
     g.iota(T.pi[:], [[1, 1]], 0, 1).then_inc(S.sg, 1)
-    G = ("sg", 2)
+    g.iota(T.xi[:], [[1, 264]], 0, 0).then_inc(S.sg, 1)
     pk, pf, tc = T.pk, T.pf, T.tc
 
     def k1(b, i):
         return b[:, i:i + 1]
-    d = []
     for i, (sh, mk) in enumerate([(0, 1), (1, 1), (2, 1), (3, 1), (0, 15), (0, 112), (0, 127)]):
-        d.append(ts(k1(pk, i), T.pi[:], sh, A.logical_shift_right, mk, A.bitwise_and, G))
-    dx = copy(T.xf[:], T.xi[:, 0:144], G)
-    dp = copy(pf[:, 0:7], pk[:, 0:7], d[-1])
+        d = ts(k1(pk, i), T.pi[:], sh, A.logical_shift_right, mk, A.bitwise_and, ("sg", 1))
+    dp = copy(pf[:, 0:7], pk[:, 0:7], d)
+    dx = copy(T.xf[:], T.xi[:, 0:144], ("sg", 2))
     ts(k1(tc, 0), k1(pf, 1), 3.0, A.mult, 1.0, A.add, dp)
     ts(k1(tc, 1), k1(pf, 2), 15.0, A.mult, 1.0, A.add, dp)
     t2 = ts(k1(tc, 2), k1(pf, 3), 255.0, A.mult, 1.0, A.add, dp)
-    d15 = ts(k1(tc, 3), k1(pf, 5), 15.0, A.add, None, None, dp)
+    ts(k1(tc, 3), k1(pf, 5), 15.0, A.add, None, None, dp)
     t3 = tt(k1(tc, 4), k1(tc, 0), k1(tc, 1), A.mult, t2)
     t4 = tt(k1(tc, 5), k1(tc, 4), k1(tc, 2), A.mult, t3)
     t5 = tt(k1(tc, 6), k1(tc, 5), k1(pf, 0), A.mult, t4)
     t6 = tt(k1(tc, 7), k1(tc, 5), k1(tc, 6), A.subtract, t5)
     ts(T.E1[:], T.xf[:], k1(tc, 3), A.is_equal, k1(tc, 6), A.mult, t6)
-    dE = ts(T.E0[:], T.xf[:], k1(tc, 3), A.is_equal, k1(tc, 7), A.mult, t6)
+    ts(T.E0[:], T.xf[:], k1(tc, 3), A.is_equal, k1(tc, 7), A.mult, t6)
     dE = ts(T.Id[:], T.xf[:, 0:128], k1(pf, 6), A.is_equal, None, None, dx)
     fill(T.zz[:], 0.0)
-    fill(T.W[:, 4096:4104], -2040.0)
-    dS0 = fill(T.sc[:], 0.0)
+    fill(T.W[:, 4096:4104], -2048.0)
+    dS0 = ts(T["wl%d" % rank][:, 0:1028:257], T.xi[:, 0:4], 0.0, A.mult, -2048.0, A.add)
 
-    cb, ce, pkd, hd = [], [], None, None
-    NP = 4
-    pw = 4096 // NP
-    na = pw // 16
-
-    def rest_of_constants():
-        ts(T.ES[:], T.xf[:], k1(tc, 3), A.is_equal, 4.0, A.mult, dx)
+    def constants_1():
+        ts(T.Ih[:], T.xf[:, 0:128], k1(pf, 6), A.is_equal, None, None)
+        ts(T.ES[:], T.xf[:], k1(tc, 3), A.is_equal, 4.0, A.mult)
         a = ts(T.xg[:], T.xi[:, 0:128], 112, A.bitwise_and, None, None)
         ts(T.BO[:], T.xg[:], k1(pf, 5), A.is_equal, None, None, a)
         ts(T.Lt[:], T.xf[:, 0:16], k1(pf, 4), A.is_gt, None, None)
@@ -143,6 +138,8 @@ def rank_program(g, core, T, topo):
         a = ts(T.m0f[:, 64:128], T.m0i[:, 64:128], 1.0, A.add, None, None, a)
         a = tt(T.m0f[:, 0:64], T.m0f[:, 0:64], T.m0f[:, 64:128], A.mult, a)
         ts(T.M0[:], T.m0f[:, 0:64], -1.0, A.add, None, None, a)
+
+    def constants_2():
         a = ts(T.jq[:], T.xi[:], 15, A.bitwise_and, None, None)
         ts(T.km[:], T.jq[:], k1(pf, 4), A.is_equal, -6144.0, A.mult, a)
         ts(k1(tc, 8), k1(pf, 3), -448.0, A.mult, 448.0, A.add)
@@ -159,36 +156,53 @@ def rank_program(g, core, T, topo):
             for i, col in enumerate([20, 12, 14]):
                 ts(T["dm%d" % (2 * i + par)][:], T.xf[:, 0:128], k1(pf, 6), A.is_equal, k1(tc, col + par), A.mult, b)
             end = 257 if par == 0 else 256
-            b2 = ts(T.km[:, par:end:2], T.km[:, par:end:2], k1(tc, 16 + par), A.add, 2048.0, A.add, b)
+            ts(T.km[:, par:end:2], T.km[:, par:end:2], k1(tc, 16 + par), A.add, 2048.0, A.add, b)
+
+    def constants_3():
         waits(vec, "sv", [("ldp", 32)])
         ts(T.cl[:], T.pats_s[:], 1048577.0, A.mult, -4.0 * KC, A.add)
         ts(T.st4[:], T.st_s[:], 4.0, A.mult, None, None)
         return ts(T.cz[:], T.pats_s[:, 0:32], 1048577.0, A.mult, None, None)
 
-    for j in range(NP):
-        sl = slice(pw * j, pw * (j + 1))
-        c = copy(T.Xb[:, sl], T.X[:, sl], ("ld%d" % (j * 2 // NP), 256))
-        e = activ(T.Xe[:, sl], T.Xb[:, sl], F.Exp, [c], scale=math.log(32.0))
+    cd, ed = [], []
+    constants_1()
+    for j in range(4):
+        if j == 2:
+            constants_2()
+        sl = slice(1024 * j, 1024 * (j + 1))
+        cd.append(copy(T.Xb[:, sl], T.X[:, sl], ("ld%d" % (j // 2), 256)))
+        ed.append(activ(T.Xe[:, sl], T.Xb[:, sl], F.Exp, [cd[-1]], scale=math.log(32.0)))
+    for j in range(4):
         items = []
         for h, E in enumerate((T.E0, T.E1)):
             for q in range(16):
-                items.append((T.psw[:, 256 * h + na * j:256 * h + na * (j + 1)], E[:, 15 - q:143 - q], T.Xb[:, pw * j + q:pw * (j + 1):16], q == 0, q == 15))
-        pkd = mms(items, [dE, c])
-        items = [(T.psh[:, na * j:na * (j + 1)], T.Id[:], T.Xe[:, pw * j + q:pw * (j + 1):16], q == 0, q == 15) for q in range(16)]
-        hd = mms(items, [e])
-    dK = rest_of_constants()
-
-    def send(buf, land, sem, deps):
-        waits(g, "gq", deps)
-        ids = [DstId(rid=topo.addr(p)[0], pnc=topo.addr(p)[1]) for p in peers]
-        g.remote_dma_fused([RemoteDMATransfer(dst_ids=ids, dma_engine_mask=topo.mask(core, peers[0]), remote_sem=S[sem], srcs=[buf[:]], dsts=[T[land][:] for _ in peers])], local_sem=S.ls)
+                items.append((T.psw[:, 256 * h + 64 * j:256 * h + 64 * (j + 1)], E[:, 15 - q:143 - q], T.Xb[:, 1024 * j + q:1024 * (j + 1):16], q == 0, q == 15))
+        pkd = mms(items, [dE, cd[j]])
+    hd = mms([(T.psh[:, 0:256], T.Id[:], T.Xe[:, q:4096:16], q == 0, q == 15) for q in range(16)], [ed[3]])
 
     ne = len(topo.engines(core, peers[0]))
-    cw = copy(T.wd[:], T.psw[:], pkd)
-    send(T.wd, "vl%d" % rank, "v%d" % rank, [cw])
-    own = copy(T.wi[:, 512 * rank:512 * rank + 512], T.psw[:])
 
-    def lists_a(h, src):
+    def send(buf, sem, deps):
+        waits(g, "gq", deps)
+        ids = [DstId(rid=topo.addr(p)[0], pnc=topo.addr(p)[1]) for p in peers]
+        g.remote_dma_fused([RemoteDMATransfer(dst_ids=ids, dma_engine_mask=topo.mask(core, peers[0]), remote_sem=S[sem], srcs=[T[buf][:]], dsts=[T[buf][:] for _ in peers])], local_sem=S.ls)
+
+    def unpack(r, ks, dep):
+        for k in ks:
+            ts(T.V[:, 4096 * r + 512 * k:4096 * r + 512 * k + 512], T.wi[:, 512 * r:512 * r + 512], 2 * k, A.logical_shift_right, 3, A.bitwise_and, dep)
+
+    def widen(r, banks, deps):
+        return mms([(T[banks[c // 2]][:, 256 * (c % 2):256 * (c % 2) + 256], T.Ih[:], T["wl%d" % r][:, 257 * c:257 * c + 256], True, True) for c in range(4)], deps)
+
+    def store(r, banks, m):
+        for c in range(4):
+            e = activ(T.W[:, 1024 * c + 256 * r:1024 * c + 256 * r + 256], T[banks[c // 2]][:, 256 * (c % 2):256 * (c % 2) + 256], F.Copy, [m])
+        return e
+
+    def totals(r, *deps):
+        return ts(T.rt[:, r::4], T["wl%d" % r][:, 256:1028:257], 2048.0, A.add, None, None, *deps)
+
+    def lists(h, src):
         z, la, ua, lb, ub = T["z%d" % h], T["la%d" % h], T["ua%d" % h], T["lb%d" % h], T["ub%d" % h]
         ts(la[:, 0:32], z[:], 63, A.bitwise_and, None, None, src)
         a = ts(la[:, 32:64], z[:], 14, A.logical_shift_right, None, None, src)
@@ -200,55 +214,58 @@ def rank_program(g, core, T, topo):
         rb = copy(ub[:], lb[:, 0:64], b)
         return ra, rb
 
-    def masks(h, ra, dep1):
-        m0 = activ(T["r0%d" % h][:], T.M0[:].indirect(T["ua%d" % h][:, 0:32]), F.Copy, [ra])
-        m1 = activ(T["r1%d" % h][:], T.M1[:, 0:257].indirect(T["ua%d" % h][:, 32:64]), F.Copy, [ra] + dep1)
-        return m0, m1
+    def mask0(h, ra):
+        return activ(T["r0%d" % h][:], T.M0[:].indirect(T["ua%d" % h][:, 0:32]), F.Copy, [ra])
 
-    a = copy(T.hi[:], T.psh[:, 0:256], hd)
+    def mask1(h, ra, *deps):
+        return activ(T["r1%d" % h][:], T.M1[:, 0:257].indirect(T["ua%d" % h][:, 32:64]), F.Copy, [ra] + list(deps))
+
+    mine = "vl%d" % rank
+    cw = copy(T[mine][:], T.psw[:], pkd)
+    send(mine, "v%d" % rank, [cw])
+    own = copy(T.wi[:, 512 * rank:512 * rank + 512], T.psw[:])
+    unpack(rank, range(0, 4), own)
+
+    mine = "wl%d" % rank
+    dh = a = copy(T.hi[:], T.psh[:, 0:256], hd)
     for c in range(4):
         b = ts(T.ni[:, 256 * c:256 * c + 256], T.hi[:], 5 * c, A.logical_shift_right, 31, A.bitwise_and, a)
     b = copy(T.nf[:], T.ni[:], b)
     for c in range(4):
-        s = op(vec, "sv", vec.tensor_tensor_scan, (T.sc[:, 258 * c + 1:258 * c + 257], T.nf[:, 256 * c:256 * c + 256], T.zz[:], 0.0, A.add, A.add), (b, dS0))
-    cs = copy(T.su[:], T.sc[:], s)
-    send(T.su, "wl%d" % rank, "w%d" % rank, [cs])
+        s = op(vec, "sv", vec.tensor_tensor_scan, (T[mine][:, 257 * c + 1:257 * c + 257], T.nf[:, 256 * c:256 * c + 256], T.zz[:], -2048.0, A.add, A.add), (b, dS0))
+    send(mine, "w%d" % rank, [s])
+    one, two = ("psw", "psh"), ("pa", "pb")
+    store(rank, one, widen(rank, one, [s, own, dh]))
 
-    def unpack(r, dep):
-        x = None
-        for k in range(8):
-            x = ts(T.V[:, 4096 * r + 512 * k:4096 * r + 512 * k + 512], T.wi[:, 512 * r:512 * r + 512], 2 * k, A.logical_shift_right, 3, A.bitwise_and, dep)
-        return x
-
-    def counts(r, src):
-        for c in range(4):
-            ts(T.W[:, 1024 * c + 256 * r:1024 * c + 256 * r + 256], src[:, 258 * c:258 * c + 256], -2040.0, A.add, None, None)
-        return copy(T.rt[:, r::4], src[:, 256::258])
-
-    counts(rank, T.sc)
-    unpack(rank, own)
-    zr = []
-    for h in range(2):
-        zr.append(tt(T["z%d" % h][:], T.st4[:, 32 * h:32 * h + 32], T.cz[:], A.add, dK))
-    la = [lists_a(h, zr[h]) for h in range(2)]
-    order = [(rank + NR - dd) % NR for dd in range(1, NR)]
-    for r in order:
+    dK = constants_3()
+    zr = [tt(T["z%d" % h][:], T.st4[:, 32 * h:32 * h + 32], T.cz[:], A.add, dK) for h in range(2)]
+    la = [lists(h, zr[h]) for h in range(2)]
+    mk = [[mask0(h, la[h][0]), None] for h in range(2)]
+    unpack(rank, range(4, 8), own)
+    totals(rank, s)
+    order = [(rank + NR - k) % NR for k in range(1, NR)]
+    last = order[2]
+    for r in order[:2]:
         x = copy(T.wi[:, 512 * r:512 * r + 512], T["vl%d" % r][:], ("v%d" % r, ne))
-        dV = unpack(r, x)
+        unpack(r, range(8), x)
+    x = copy(T.wi[:, 512 * last:512 * last + 512], T["vl%d" % last][:], ("v%d" % last, ne))
+    unpack(last, range(0, 2), x)
     for r in order:
-        waits(vec, "sv", [("w%d" % r, ne)])
-        dR = counts(r, T["wl%d" % r])
+        dR = totals(r, ("w%d" % r, ne))
     a = op(vec, "sv", vec.tensor_tensor_scan, (T.inc[:], T.rt[:], T.zz[:, 0:16], 0.0, A.add, A.add), (dR,))
     copy(T.bs[:, 256:257], T.inc[:, 15:16], a)
     a = tt(T.exc[:], T.inc[:], T.rt[:], A.subtract, a)
-    bd = []
-    for k in range(16):
-        o, s1, s2 = T.bs[:, 16 * k:16 * k + 16], T.rt[:, k:k + 1], T.exc[:, k:k + 1]
-        if k % 3 == 2:
-            bd.append(activ(o, T.Lt[:], F.Identity, [a], bias=s2, scale=s1))
-        else:
-            bd.append(ts(o, T.Lt[:], s1, A.mult, s2, A.add, a))
-    m = mms([(T.psm[:, 0:257], T.BO[:], T.bs[:, 0:257], True, True)], [bd[-1], bd[-2]])
+    for k in range(10, 16):
+        ba = activ(T.bs[:, 16 * k:16 * k + 16], T.Lt[:], F.Identity, [a], bias=k1(T.exc, k), scale=k1(T.rt, k))
+    for k in range(10):
+        b = ts(T.bs[:, 16 * k:16 * k + 16], T.Lt[:], k1(T.rt, k), A.mult, k1(T.exc, k), A.add, a)
+    m = mms([(T.psm[:, 0:257], T.BO[:], T.bs[:, 0:257], True, True)], [b, ba])
+    free = ("sa", cnt["sa"])
+    w1 = widen(order[0], one, [("w%d" % order[0], ne), free])
+    w2 = widen(order[1], two, [("w%d" % order[1], ne)])
+    free = store(order[0], one, w1)
+    store(order[1], two, w2)
+    unpack(last, range(2, 5), x)
     a = copy(T.bi[:, 0:257], T.psm[:, 0:257], m)
     ts(T.dg[:, 0:257], T.bi[:, 0:257], 11, A.logical_shift_right, None, None, a)
     ts(T.dg[:, 257:514], T.bi[:, 0:257], 2046, A.bitwise_and, None, None, a)
@@ -256,12 +273,17 @@ def rank_program(g, core, T, topo):
     a = copy(T.df[:, 0:771], T.dg[:, 0:771], a)
     for par in range(2):
         n = 129 - par
-        m = mms([(T.psd[:, 256 * par:256 * par + n], T["dm%d" % (2 * i + par)][:], T.df[:, 257 * i + par:257 * i + 257:2], i == 0, i == 2) for i in range(3)], [a])
+        m = mms([(T.psd[:, 256 * par + par:256 * par + par + n] if par == 0 else T.psm[:, 0:n], T["dm%d" % (2 * i + par)][:], T.df[:, 257 * i + par:257 * i + 257:2], i == 0, i == 2) for i in range(3)], [a])
+    w3 = widen(last, one, [("w%d" % last, ne), free])
+    unpack(last, range(5, 8), x)
     for par in range(2):
         n, end = 129 - par, 257 if par == 0 else 256
-        dM = tt(T.M1[:, par:end:2], T.psd[:, 256 * par:256 * par + n], T.km[:, par:end:2], A.add, m)
+        dM = tt(T.M1[:, par:end:2], (T.psd if par == 0 else T.psm)[:, 0:n], T.km[:, par:end:2], A.add, m)
+    mk[0][1] = mask1(0, la[0][0], dM)
+    dW = store(last, one, w3)
+    mk[1][1] = mask1(1, la[1][0], dM)
+    dV = ("sv", cnt["sv"])
 
-    mk = [masks(h, la[h][0], [dM]) for h in range(2)]
     lb = [la[0][1], la[1][1]]
     res = [None, None]
 
@@ -270,31 +292,34 @@ def rank_program(g, core, T, topo):
         return mms(items, [dep])
 
     def y1(h):
-        d = tt(T["ya%d" % h][:], T.V[:].indirect(T["ub%d" % h][:, 0:32]), T["r0%d" % h][:], A.is_equal, lb[h], mk[h][0])
-        sums(h, "ya%d" % h, True, d)
+        e = tt(T["ya%d" % h][:], T.V[:].indirect(T["ub%d" % h][:, 0:32]), T["r0%d" % h][:], A.is_equal, lb[h], mk[h][0], dV)
+        sums(h, "ya%d" % h, True, e)
 
     def y2(h):
-        d = tt(T["yb%d" % h][:], T.W[:, 0:4097].indirect(T["ub%d" % h][:, 32:64]), T["r1%d" % h][:], A.max, lb[h], mk[h][1])
-        res[h] = sums(h, "yb%d" % h, False, d)
+        e = tt(T["yb%d" % h][:], T.W[:, 0:4097].indirect(T["ub%d" % h][:, 32:64]), T["r1%d" % h][:], A.max, lb[h], mk[h][1], dW)
+        res[h] = sums(h, "yb%d" % h, False, e)
 
     def nxt(h, t):
         z = tt(T["z%d" % h][:], T["ps%d" % h][:, 0:32], T.cl[:, 32 * t:32 * t + 32], A.add, res[h])
-        ra, rb = lists_a(h, z)
-        lb[h] = rb
-        mk[h] = masks(h, ra, [])
+        ra, lb[h] = lists(h, z)
+        mk[h] = [mask0(h, ra), mask1(h, ra)]
 
-    for t in range(ST):
+    y1(0)
+    y1(1)
+    y2(0)
+    y2(1)
+    nxt(0, 1)
+    for t in range(1, ST):
         y1(0)
-        if t:
-            nxt(1, t)
+        nxt(1, t)
         y2(0)
         y1(1)
         if t + 1 < ST:
             nxt(0, t + 1)
         y2(1)
     for h in range(2):
-        d = ts(T["yo%d" % h][:], T["ps%d" % h][:, 0:32], 0.25, A.mult, -float(KC), A.add, res[h])
-        waits(syn, "sy", [d])
+        e = ts(T["yo%d" % h][:], T["ps%d" % h][:, 0:32], 0.25, A.mult, -float(KC), A.add, res[h])
+        waits(syn, "sy", [e])
         syn.dma_start(T.y[:, 32 * h:32 * h + 32], T["yo%d" % h][:]).then_inc(S["yd%d" % h], 16)
     waits(syn, "sy", [("yd0", 16), ("yd1", 16)])
     g.wait_ge(S.ls, 2 * ne)

@@ -6,19 +6,22 @@ from concourse.mybir import AluOpType as A, ActivationFunctionType as F
 NR, ST = 4, 8
 KC = 30718 - 2048
 SCRATCH = {
-    "X": ("sbuf", [128, 4096], "int32"), "Xb": ("sbuf", [128, 4096], "bfloat16"), "Xe": ("sbuf", [128, 4096], "bfloat16"),
-    "V": ("sbuf", [128, 16384], "int32"), "W": ("sbuf", [128, 4104], "float32"),
+    "Xb": ("sbuf", [128, 4096], "bfloat16"), "Xe": ("sbuf", [128, 4096], "bfloat16"),
+    "V": ("sbuf", [128, 16392], "int32"), "W": ("sbuf", [128, 4104], "float32"),
     "wi": ("sbuf", [128, 2048], "int32"),
-    "hi": ("sbuf", [128, 256], "int32"), "ni": ("sbuf", [128, 1024], "int32"), "nf": ("sbuf", [128, 1024], "float32"),
-    "zz": ("sbuf", [128, 256], "float32"),
+    "hi": ("sbuf", [128, 256], "int32"), "ni": ("sbuf", [128, 768], "int32"), "nf": ("sbuf", [128, 768], "float32"),
+    "zz": ("sbuf", [128, 256], "float32"), "kt": ("sbuf", [128, 256], "float16"),
     "rt": ("sbuf", [128, 16], "float32"), "inc": ("sbuf", [128, 16], "float32"), "exc": ("sbuf", [128, 16], "float32"),
-    "bs": ("sbuf", [128, 264], "float32"), "bi": ("sbuf", [128, 264], "int32"),
-    "dg": ("sbuf", [128, 792], "int32"), "df": ("sbuf", [128, 792], "float16"), "M1": ("sbuf", [128, 264], "float32"),
+    "tq": ("sbuf", [128, 8], "float32"),
+    "bs": ("sbuf", [128, 264], "float32"),
+    "dh": ("sbuf", [128, 264], "float16"), "dr": ("sbuf", [128, 264], "float16"), "de": ("sbuf", [128, 264], "float16"),
+    "M1": ("sbuf", [128, 264], "float32"),
     "M0": ("sbuf", [128, 64], "bfloat16"), "km": ("sbuf", [128, 264], "float32"), "jq": ("sbuf", [128, 264], "int32"),
     "xi": ("sbuf", [128, 264], "int32"), "xf": ("sbuf", [128, 144], "float32"), "pi": ("sbuf", [128, 1], "int32"),
-    "pk": ("sbuf", [128, 8], "int32"), "pf": ("sbuf", [128, 8], "float32"), "tc": ("sbuf", [128, 32], "float32"),
-    "E0": ("sbuf", [128, 144], "bfloat16"), "E1": ("sbuf", [128, 144], "bfloat16"), "ES": ("sbuf", [128, 144], "float16"),
-    "Id": ("sbuf", [128, 128], "bfloat16"), "Ih": ("sbuf", [128, 128], "float16"),
+    "pk": ("sbuf", [128, 8], "int32"), "pf": ("sbuf", [128, 8], "float32"), "tc": ("sbuf", [128, 40], "float32"),
+    "w4": ("sbuf", [128, 1], "float32"),
+    "E": ("sbuf", [128, 144], "bfloat16"), "ES": ("sbuf", [128, 144], "float16"),
+    "Pm": ("sbuf", [128, 128], "bfloat16"), "Ih": ("sbuf", [128, 128], "float16"), "In": ("sbuf", [128, 128], "float16"),
     "xg": ("sbuf", [128, 128], "int32"), "BO": ("sbuf", [128, 128], "float32"),
     "Lt": ("sbuf", [128, 16], "float32"), "m0i": ("sbuf", [128, 128], "int32"), "m0f": ("sbuf", [128, 128], "float32"),
     "pats_s": ("sbuf", [128, 256], "int32"), "st_s": ("sbuf", [128, 64], "int32"), "cl": ("sbuf", [128, 256], "float32"),
@@ -27,23 +30,25 @@ SCRATCH = {
     "psd": ("psum", [128, 512], "float32"), "pa": ("psum", [128, 512], "float32"), "pb": ("psum", [128, 512], "float32"),
 }
 for _k in range(NR):
-    SCRATCH["vl%d" % _k] = ("sbuf", [128, 512], "uint16")
-    SCRATCH["wl%d" % _k] = ("sbuf", [128, 1028], "float16")
+    SCRATCH["wl%d" % _k] = ("sbuf", [128, 772], "float16")
+    for _h in range(2):
+        SCRATCH["vl%d%d" % (_k, _h)] = ("sbuf", [128, 256], "uint16")
 for _k in range(6):
     SCRATCH["dm%d" % _k] = ("sbuf", [128, 128], "float16")
 for _h in range(2):
     SCRATCH["ps%d" % _h] = ("psum", [128, 512], "float32")
     SCRATCH["z%d" % _h] = ("sbuf", [128, 32], "int32")
     SCRATCH["la%d" % _h] = ("sbuf", [128, 64], "int32")
-    SCRATCH["lb%d" % _h] = ("sbuf", [128, 96], "int32")
+    SCRATCH["lb%d" % _h] = ("sbuf", [128, 64], "int32")
     SCRATCH["ua%d" % _h] = ("sbuf", [128, 64], "uint16")
-    SCRATCH["ub%d" % _h] = ("sbuf", [128, 64], "uint16")
+    SCRATCH["um%d" % _h] = ("sbuf", [128, 32], "uint16")
+    SCRATCH["uv%d" % _h] = ("sbuf", [128, 32], "uint16")
     SCRATCH["r0%d" % _h] = ("sbuf", [128, 512], "bfloat16")
     SCRATCH["r1%d" % _h] = ("sbuf", [128, 512], "float32")
     SCRATCH["ya%d" % _h] = ("sbuf", [128, 512], "float16")
     SCRATCH["yb%d" % _h] = ("sbuf", [128, 512], "float16")
     SCRATCH["yo%d" % _h] = ("sbuf", [128, 32], "float32")
-SEMAPHORES = ["sv", "sa", "st", "sg", "ls", "ld0", "ld1", "ldp", "yd0", "yd1"] + ["v%d" % k for k in range(NR)] + ["w%d" % k for k in range(NR)]
+SEMAPHORES = ["sv", "sa", "st", "sg", "ls", "gx0", "gx1", "ldp", "yd0", "yd1"] + ["w%d" % k for k in range(NR)] + ["v%d%d" % (k, h) for k in range(NR) for h in range(2)]
 
 
 def rank_program(g, core, T, topo):
@@ -94,44 +99,43 @@ def rank_program(g, core, T, topo):
         cnt["st"] += 1
         return ("st", cnt["st"])
 
-    for j in range(2):
-        for w in range(16):
-            q = syn if w % 2 == 0 else act
-            q.dma_start(T.X[w::16, 2048 * j:2048 * (j + 1)], T.bwt[:, 4096 * w + 2048 * j:4096 * w + 2048 * (j + 1)]).then_inc(S["ld%d" % j], 16)
+    def load(h):
+        g.dma_start(T.Xb[64 * h:64 * h + 64, :], T.bwt[:, 32768 * h:32768 * h + 32768]).then_inc(S["gx%d" % h], 16)
+    load(0)
+    g.iota(T.pi[:], [[1, 1]], 0, 1).then_inc(S.sg, 1)
+    g.iota(T.xi[:], [[1, 264]], 0, 0).then_inc(S.sg, 1)
+    load(1)
     syn.dma_start(T.pats_s[:], T.pats[:]).then_inc(S.ldp, 16)
     syn.dma_start(T.st_s[:], T.starts[:]).then_inc(S.ldp, 16)
 
-    g.iota(T.pi[:], [[1, 1]], 0, 1).then_inc(S.sg, 1)
-    g.iota(T.xi[:], [[1, 264]], 0, 0).then_inc(S.sg, 1)
     pk, pf, tc = T.pk, T.pf, T.tc
 
     def k1(b, i):
         return b[:, i:i + 1]
-    for i, (sh, mk) in enumerate([(0, 1), (1, 1), (2, 1), (3, 1), (0, 15), (0, 112), (0, 127)]):
+    for i, (sh, mk) in enumerate([(0, 1), (0, 7), (0, 56), (3, 1), (0, 15), (0, 112), (0, 127), (0, 64)]):
         d = ts(k1(pk, i), T.pi[:], sh, A.logical_shift_right, mk, A.bitwise_and, ("sg", 1))
-    dp = copy(pf[:, 0:7], pk[:, 0:7], d)
+    dp = copy(pf[:, 0:8], pk[:, 0:8], d)
+    dw = activ(T.w4[:], k1(pf, 1), F.Exp, [dp], scale=math.log(4.0))
     dx = copy(T.xf[:], T.xi[:, 0:144], ("sg", 2))
-    ts(k1(tc, 0), k1(pf, 1), 3.0, A.mult, 1.0, A.add, dp)
-    ts(k1(tc, 1), k1(pf, 2), 15.0, A.mult, 1.0, A.add, dp)
-    t2 = ts(k1(tc, 2), k1(pf, 3), 255.0, A.mult, 1.0, A.add, dp)
-    ts(k1(tc, 3), k1(pf, 5), 15.0, A.add, None, None, dp)
-    t3 = tt(k1(tc, 4), k1(tc, 0), k1(tc, 1), A.mult, t2)
-    t4 = tt(k1(tc, 5), k1(tc, 4), k1(tc, 2), A.mult, t3)
-    t5 = tt(k1(tc, 6), k1(tc, 5), k1(pf, 0), A.mult, t4)
-    t6 = tt(k1(tc, 7), k1(tc, 5), k1(tc, 6), A.subtract, t5)
-    ts(T.E1[:], T.xf[:], k1(tc, 3), A.is_equal, k1(tc, 6), A.mult, t6)
-    ts(T.E0[:], T.xf[:], k1(tc, 3), A.is_equal, k1(tc, 7), A.mult, t6)
-    dE = ts(T.Id[:], T.xf[:, 0:128], k1(pf, 6), A.is_equal, None, None, dx)
+    ts(k1(tc, 3), k1(pf, 2), 2.0, A.mult, 15.0, A.add, dp)
+    b = ts(k1(tc, 4), k1(pf, 7), 0.125, A.mult, k1(pf, 1), A.add)
+    ts(k1(tc, 5), k1(pf, 5), 15.0, A.add, None, None)
+    b = ts(k1(tc, 6), k1(pf, 2), 2.0, A.mult, k1(tc, 4), A.add, b)
+    dE = ts(T.E[:], T.xf[:], k1(tc, 3), A.is_equal, T.w4[:], A.mult, b, dx, dw)
+    dP = ts(T.Pm[:], T.xf[:, 0:128], k1(tc, 6), A.is_equal, None, None, b)
     fill(T.zz[:], 0.0)
+    fill(T.V[:, 16384:16392], 9)
     fill(T.W[:, 4096:4104], -2048.0)
-    dS0 = ts(T["wl%d" % rank][:, 0:1028:257], T.xi[:, 0:4], 0.0, A.mult, -2048.0, A.add)
+    dS0 = ts(T["wl%d" % rank][:, 0:772:257], T.xi[:, 0:4], 0.0, A.mult, -2048.0, A.add)
 
     def constants_1():
         ts(T.Ih[:], T.xf[:, 0:128], k1(pf, 6), A.is_equal, None, None)
-        ts(T.ES[:], T.xf[:], k1(tc, 3), A.is_equal, 4.0, A.mult)
+        ts(T.In[:], T.xf[:, 0:128], k1(pf, 6), A.is_equal, -1.0, A.mult)
+        ts(T.kt[:], T.xi[:, 0:256], 16.0, A.mult, -8192.0, A.add)
+        ts(T.ES[:], T.xf[:], k1(tc, 5), A.is_equal, 4.0, A.mult)
         a = ts(T.xg[:], T.xi[:, 0:128], 112, A.bitwise_and, None, None)
-        ts(T.BO[:], T.xg[:], k1(pf, 5), A.is_equal, None, None, a)
         ts(T.Lt[:], T.xf[:, 0:16], k1(pf, 4), A.is_gt, None, None)
+        ts(T.BO[:], T.xg[:], k1(pf, 5), A.is_equal, 1.0 / 2048, A.mult, a)
         ts(T.m0i[:, 0:64], T.xi[:, 0:64], 2, A.logical_shift_right, None, None)
         a = ts(T.m0i[:, 64:128], T.xi[:, 0:64], 3, A.bitwise_and, None, None)
         ts(T.m0f[:, 0:64], T.m0i[:, 0:64], k1(pf, 4), A.is_gt, None, None, a)
@@ -141,44 +145,48 @@ def rank_program(g, core, T, topo):
 
     def constants_2():
         a = ts(T.jq[:], T.xi[:], 15, A.bitwise_and, None, None)
-        ts(T.km[:], T.jq[:], k1(pf, 4), A.is_equal, -6144.0, A.mult, a)
         ts(k1(tc, 8), k1(pf, 3), -448.0, A.mult, 448.0, A.add)
         for i, v in enumerate([9, 8]):
             ts(k1(tc, 10 + i), k1(pf, 4), float(v), A.is_equal, 256.0, A.mult)
         for i, v in enumerate([11, 10, 13, 12]):
-            ts(k1(tc, 12 + i), k1(pf, 4), float(v), A.is_equal, None, None)
-        for i, v in enumerate([13, 12]):
-            a = ts(k1(tc, 16 + i), k1(pf, 4), float(v), A.is_equal, -2.0, A.mult)
+            a = ts(k1(tc, 12 + i), k1(pf, 4), float(v), A.is_equal, None, None)
         b = tt(k1(tc, 18), k1(tc, 8), k1(pf, 0), A.mult, a)
+        ts(T.km[:], T.jq[:], k1(pf, 4), A.is_equal, -6144.0, A.mult)
         b = tt(k1(tc, 19), k1(tc, 8), k1(tc, 18), A.subtract, b)
+        c = ts(tc[:, 22:24], tc[:, 12:14], -2048.0, A.mult, 2048.0, A.add)
         b = tt(tc[:, 20:22], tc[:, 18:20], tc[:, 10:12], A.add, b)
+        d = ts(tc[:, 24:26], tc[:, 14:16], 2046.0, A.mult, None, None)
+        e = tt(tc[:, 26:28], tc[:, 12:14], tc[:, 14:16], A.subtract)
+        ts(tc[:, 28:30], tc[:, 14:16], 2048.0, A.mult, None, None)
+        f = ts(tc[:, 30:32], tc[:, 20:22], -1025.0, A.mult, None, None, b)
+        d = tt(tc[:, 22:24], tc[:, 22:24], tc[:, 24:26], A.add, c, d)
+        for i, col in enumerate([20, 26, 28]):
+            for par in range(2):
+                b = ts(T["dm%d" % (2 * i + par)][:], T.xf[:, 0:128], k1(pf, 6), A.is_equal, k1(tc, col + par), A.mult, f)
+        d = tt(tc[:, 32:34], tc[:, 22:24], tc[:, 30:32], A.add, d, f)
         for par in range(2):
-            for i, col in enumerate([20, 12, 14]):
-                ts(T["dm%d" % (2 * i + par)][:], T.xf[:, 0:128], k1(pf, 6), A.is_equal, k1(tc, col + par), A.mult, b)
             end = 257 if par == 0 else 256
-            ts(T.km[:, par:end:2], T.km[:, par:end:2], k1(tc, 16 + par), A.add, 2048.0, A.add, b)
+            ts(T.km[:, par:end:2], T.km[:, par:end:2], k1(tc, 32 + par), A.add, None, None, d)
 
     def constants_3():
         waits(vec, "sv", [("ldp", 32)])
         ts(T.cl[:], T.pats_s[:], 1048577.0, A.mult, -4.0 * KC, A.add)
+        for h in range(2):
+            ts(T["uv%d" % h][:], T.st_s[:, 32 * h:32 * h + 32], 1.0 / 16, A.mult, -15.0 / 32, A.add)
         ts(T.st4[:], T.st_s[:], 4.0, A.mult, None, None)
         return ts(T.cz[:], T.pats_s[:, 0:32], 1048577.0, A.mult, None, None)
 
-    cd, ed = [], []
     constants_1()
+    dK = constants_3()
+    ld = [("gx0", 16), ("gx1", 16)]
+    pkd = []
+    for h, bank in enumerate(("psw", "pa")):
+        sl = slice(64 * h, 64 * h + 64)
+        pkd.append(mms([(T[bank][:, 0:256], T.E[sl, 15 - q:143 - q], T.Xb[sl, q:4096:16], q == 0, q == 15) for q in range(16)], [dE, ld[h]]))
     for j in range(4):
-        if j == 2:
-            constants_2()
         sl = slice(1024 * j, 1024 * (j + 1))
-        cd.append(copy(T.Xb[:, sl], T.X[:, sl], ("ld%d" % (j // 2), 256)))
-        ed.append(activ(T.Xe[:, sl], T.Xb[:, sl], F.Exp, [cd[-1]], scale=math.log(32.0)))
-    for j in range(4):
-        items = []
-        for h, E in enumerate((T.E0, T.E1)):
-            for q in range(16):
-                items.append((T.psw[:, 256 * h + 64 * j:256 * h + 64 * (j + 1)], E[:, 15 - q:143 - q], T.Xb[:, 1024 * j + q:1024 * (j + 1):16], q == 0, q == 15))
-        pkd = mms(items, [dE, cd[j]])
-    hd = mms([(T.psh[:, 0:256], T.Id[:], T.Xe[:, q:4096:16], q == 0, q == 15) for q in range(16)], [ed[3]])
+        e = activ(T.Xe[:, sl], T.Xb[:, sl], F.Exp, ld, scale=math.log(32.0))
+        hd = mms([(T.psh[:, 64 * j:64 * j + 64], T.Pm[:], T.Xe[:, 1024 * j + q:1024 * (j + 1):16], q == 0, q == 15) for q in range(16)], [dP, e])
 
     ne = len(topo.engines(core, peers[0]))
 
@@ -187,12 +195,17 @@ def rank_program(g, core, T, topo):
         ids = [DstId(rid=topo.addr(p)[0], pnc=topo.addr(p)[1]) for p in peers]
         g.remote_dma_fused([RemoteDMATransfer(dst_ids=ids, dma_engine_mask=topo.mask(core, peers[0]), remote_sem=S[sem], srcs=[T[buf][:]], dsts=[T[buf][:] for _ in peers])], local_sem=S.ls)
 
-    def unpack(r, ks, dep):
-        for k in ks:
-            ts(T.V[:, 4096 * r + 512 * k:4096 * r + 512 * k + 512], T.wi[:, 512 * r:512 * r + 512], 2 * k, A.logical_shift_right, 3, A.bitwise_and, dep)
+    def unpack(r, h, k, dep):
+        o = 4096 * r + 2048 * h + 256 * k
+        ts(T.V[:, o:o + 256], T.wi[:, 512 * r + 256 * h:512 * r + 256 * h + 256], 2 * k, A.logical_shift_right, 3, A.bitwise_and, dep)
 
     def widen(r, banks, deps):
-        return mms([(T[banks[c // 2]][:, 256 * (c % 2):256 * (c % 2) + 256], T.Ih[:], T["wl%d" % r][:, 257 * c:257 * c + 256], True, True) for c in range(4)], deps)
+        def half(c):
+            return T[banks[c // 2]][:, 256 * (c % 2):256 * (c % 2) + 256]
+
+        def cnts(c):
+            return T["wl%d" % r][:, 257 * c:257 * c + 256]
+        return mms([(half(c), T.Ih[:], cnts(c), True, True) for c in range(3)] + [(half(3), T.Ih[:], T.kt[:], True, False)] + [(half(3), T.In[:], cnts(c), False, c == 2) for c in range(3)], deps)
 
     def store(r, banks, m):
         for c in range(4):
@@ -200,126 +213,151 @@ def rank_program(g, core, T, topo):
         return e
 
     def totals(r, *deps):
-        return ts(T.rt[:, r::4], T["wl%d" % r][:, 256:1028:257], 2048.0, A.add, None, None, *deps)
+        return ts(T.rt[:, r:12:4], T["wl%d" % r][:, 256:771:257], 2048.0, A.add, None, None, *deps)
 
-    def lists(h, src):
-        z, la, ua, lb, ub = T["z%d" % h], T["la%d" % h], T["ua%d" % h], T["lb%d" % h], T["ub%d" % h]
-        ts(la[:, 0:32], z[:], 63, A.bitwise_and, None, None, src)
-        a = ts(la[:, 32:64], z[:], 14, A.logical_shift_right, None, None, src)
-        ts(lb[:, 0:32], z[:], 6, A.logical_shift_right, 16383, A.bitwise_and)
-        ts(lb[:, 32:64], z[:], 6, A.logical_shift_right, 255, A.bitwise_and)
-        b = ts(lb[:, 64:96], z[:], 10, A.logical_shift_right, 0x1F00, A.bitwise_and)
-        ra = copy(ua[:], la[:], a)
-        b = tt(lb[:, 32:64], lb[:, 32:64], lb[:, 64:96], A.add, b)
-        rb = copy(ub[:], lb[:, 0:64], b)
-        return ra, rb
+    def rows(h, *deps):
+        return ts(T["um%d" % h][:], T["z%d" % h][:], 2.0 ** -14, A.mult, 2.0 ** -15 - 0.5, A.add, *deps)
 
-    def mask0(h, ra):
-        return activ(T["r0%d" % h][:], T.M0[:].indirect(T["ua%d" % h][:, 0:32]), F.Copy, [ra])
+    def parts(h):
+        ts(T["lb%d" % h][:, 0:32], T["z%d" % h][:], 6, A.logical_shift_right, 255, A.bitwise_and)
+        return ts(T["lb%d" % h][:, 32:64], T["z%d" % h][:], 10, A.logical_shift_right, 0x1F00, A.bitwise_and)
 
-    def mask1(h, ra, *deps):
-        return activ(T["r1%d" % h][:], T.M1[:, 0:257].indirect(T["ua%d" % h][:, 32:64]), F.Copy, [ra] + list(deps))
+    def rest(h, b):
+        la, lb = T["la%d" % h], T["lb%d" % h]
+        ts(la[:, 0:32], T["z%d" % h][:], 63, A.bitwise_and, None, None)
+        b = tt(la[:, 32:64], lb[:, 0:32], lb[:, 32:64], A.add, b)
+        return copy(T["ua%d" % h][:], la[:], b)
 
-    mine = "vl%d" % rank
-    cw = copy(T[mine][:], T.psw[:], pkd)
-    send(mine, "v%d" % rank, [cw])
-    own = copy(T.wi[:, 512 * rank:512 * rank + 512], T.psw[:])
-    unpack(rank, range(0, 4), own)
+    def mask0(h, u):
+        return activ(T["r0%d" % h][:], T.M0[:].indirect(T["ua%d" % h][:, 0:32]), F.Copy, [u])
+
+    def mask1(h, m, *deps):
+        return activ(T["r1%d" % h][:], T.M1[:, 0:257].indirect(T["um%d" % h][:]), F.Copy, [m] + list(deps))
+
+    constants_2()
+    own = []
+    for h, bank in enumerate(("psw", "pa")):
+        mine = "vl%d%d" % (rank, h)
+        cw = copy(T[mine][:], T[bank][:, 0:256], pkd[h])
+        send(mine, "v%d%d" % (rank, h), [cw])
+        own.append(copy(T.wi[:, 512 * rank + 256 * h:512 * rank + 256 * h + 256], T[bank][:, 0:256]))
+        for k in range(8):
+            unpack(rank, h, k, own[h])
+    zr = [tt(T["z%d" % h][:], T.st4[:, 32 * h:32 * h + 32], T.cz[:], A.add, dK) for h in range(2)]
+    um = [rows(h, zr[h]) for h in range(2)]
+    pb = [parts(h) for h in range(2)]
+    lb = [rest(h, pb[h]) for h in range(2)]
+    mk = [[mask0(h, lb[h]), None] for h in range(2)]
 
     mine = "wl%d" % rank
     dh = a = copy(T.hi[:], T.psh[:, 0:256], hd)
-    for c in range(4):
+    for c in range(3):
         b = ts(T.ni[:, 256 * c:256 * c + 256], T.hi[:], 5 * c, A.logical_shift_right, 31, A.bitwise_and, a)
     b = copy(T.nf[:], T.ni[:], b)
-    for c in range(4):
+    for c in range(3):
         s = op(vec, "sv", vec.tensor_tensor_scan, (T[mine][:, 257 * c + 1:257 * c + 257], T.nf[:, 256 * c:256 * c + 256], T.zz[:], -2048.0, A.add, A.add), (b, dS0))
     send(mine, "w%d" % rank, [s])
     one, two = ("psw", "psh"), ("pa", "pb")
-    store(rank, one, widen(rank, one, [s, own, dh]))
+    store(rank, one, widen(rank, one, [s, own[0], own[1], dh]))
 
-    dK = constants_3()
-    zr = [tt(T["z%d" % h][:], T.st4[:, 32 * h:32 * h + 32], T.cz[:], A.add, dK) for h in range(2)]
-    la = [lists(h, zr[h]) for h in range(2)]
-    mk = [[mask0(h, la[h][0]), None] for h in range(2)]
-    unpack(rank, range(4, 8), own)
-    totals(rank, s)
     order = [(rank + NR - k) % NR for k in range(1, NR)]
     last = order[2]
-    for r in order[:2]:
-        x = copy(T.wi[:, 512 * r:512 * r + 512], T["vl%d" % r][:], ("v%d" % r, ne))
-        unpack(r, range(8), x)
-    x = copy(T.wi[:, 512 * last:512 * last + 512], T["vl%d" % last][:], ("v%d" % last, ne))
-    unpack(last, range(0, 2), x)
-    for r in order:
-        dR = totals(r, ("w%d" % r, ne))
-    a = op(vec, "sv", vec.tensor_tensor_scan, (T.inc[:], T.rt[:], T.zz[:, 0:16], 0.0, A.add, A.add), (dR,))
-    copy(T.bs[:, 256:257], T.inc[:, 15:16], a)
-    a = tt(T.exc[:], T.inc[:], T.rt[:], A.subtract, a)
-    for k in range(10, 16):
-        ba = activ(T.bs[:, 16 * k:16 * k + 16], T.Lt[:], F.Identity, [a], bias=k1(T.exc, k), scale=k1(T.rt, k))
-    for k in range(10):
-        b = ts(T.bs[:, 16 * k:16 * k + 16], T.Lt[:], k1(T.rt, k), A.mult, k1(T.exc, k), A.add, a)
-    m = mms([(T.psm[:, 0:257], T.BO[:], T.bs[:, 0:257], True, True)], [b, ba])
+    jobs = [(r, h, k) for h in range(2) for r in order for k in range(8)]
+    at = {}
+
+    def work(n):
+        for r, h, k in jobs[:n]:
+            if k == 0:
+                at[r, h] = copy(T.wi[:, 512 * r + 256 * h:512 * r + 256 * h + 256], T["vl%d%d" % (r, h)][:], ("v%d%d" % (r, h), ne))
+            unpack(r, h, k, at[r, h])
+        del jobs[:n]
+
+    work(1)
+    totals(rank, s)
+    work(len(jobs) - 17)
     free = ("sa", cnt["sa"])
     w1 = widen(order[0], one, [("w%d" % order[0], ne), free])
     w2 = widen(order[1], two, [("w%d" % order[1], ne)])
     free = store(order[0], one, w1)
     store(order[1], two, w2)
-    unpack(last, range(2, 5), x)
-    a = copy(T.bi[:, 0:257], T.psm[:, 0:257], m)
-    ts(T.dg[:, 0:257], T.bi[:, 0:257], 11, A.logical_shift_right, None, None, a)
-    ts(T.dg[:, 257:514], T.bi[:, 0:257], 2046, A.bitwise_and, None, None, a)
-    a = ts(T.dg[:, 514:771], T.bi[:, 0:257], 1, A.bitwise_and, None, None, a)
-    a = copy(T.df[:, 0:771], T.dg[:, 0:771], a)
-    for par in range(2):
-        n = 129 - par
-        m = mms([(T.psd[:, 256 * par + par:256 * par + par + n] if par == 0 else T.psm[:, 0:n], T["dm%d" % (2 * i + par)][:], T.df[:, 257 * i + par:257 * i + 257:2], i == 0, i == 2) for i in range(3)], [a])
+    for r in order:
+        dR = totals(r, ("w%d" % r, ne))
+    work(1)
+    a = tt(T.tq[:, 0:4], T.rt[:, 0:4], T.rt[:, 4:8], A.add, dR)
+    work(1)
+    a = tt(T.tq[:, 4:8], T.tq[:, 0:4], T.rt[:, 8:12], A.add, a)
+    work(1)
+    a = ts(T.rt[:, 12:16], T.tq[:, 4:8], -1.0, A.mult, 4096.0, A.add, a)
+    work(1)
+    a = op(vec, "sv", vec.tensor_tensor_scan, (T.inc[:], T.rt[:], T.zz[:, 0:16], 131200.0, A.add, A.add), (a,))
+    work(1)
+    b = copy(T.bs[:, 256:257], T.inc[:, 15:16], a)
+    a = tt(T.exc[:], T.inc[:], T.rt[:], A.subtract, a)
+    work(1)
+    for k in range(9, 16):
+        ba = activ(T.bs[:, 16 * k:16 * k + 16], T.Lt[:], F.Identity, [a], bias=k1(T.exc, k), scale=k1(T.rt, k))
+    for k in range(9):
+        b = ts(T.bs[:, 16 * k:16 * k + 16], T.Lt[:], k1(T.rt, k), A.mult, k1(T.exc, k), A.add, a)
+    m = mms([(T.psm[:, 0:257], T.BO[:], T.bs[:, 0:257], True, True)], [b, ba])
     w3 = widen(last, one, [("w%d" % last, ne), free])
-    unpack(last, range(5, 8), x)
+    dW = store(last, one, w3)
+    work(6)
+    n = 257
+    a = ts(T.dh[:, 0:n], T.psm[:, 0:n], 1.0, A.mult, 2.0 ** -12 - 0.5, A.add, m)
+    work(1)
+    a = tt(T.dr[:, 0:n], T.psm[:, 0:n], T.dh[:, 0:n], A.subtract, a)
+    work(1)
+    a = ts(T.de[:, 0:n], T.dr[:, 0:n], 2048.0, A.mult, 2047.75, A.add, a)
+    for par in range(2):
+        m = mms([(T.psd[:, par:par + 129] if par == 0 else T.psm[:, 0:128], T["dm%d" % (2 * i + par)][:], T[buf][:, par:257:2], i == 0, i == 2) for i, buf in enumerate(("dh", "de", "dr"))], [a])
+    work(len(jobs))
     for par in range(2):
         n, end = 129 - par, 257 if par == 0 else 256
         dM = tt(T.M1[:, par:end:2], (T.psd if par == 0 else T.psm)[:, 0:n], T.km[:, par:end:2], A.add, m)
-    mk[0][1] = mask1(0, la[0][0], dM)
-    dW = store(last, one, w3)
-    mk[1][1] = mask1(1, la[1][0], dM)
+    mk[0][1] = mask1(0, um[0], dM)
+    mk[1][1] = mask1(1, um[1], dM)
     dV = ("sv", cnt["sv"])
 
-    lb = [la[0][1], la[1][1]]
     res = [None, None]
 
     def sums(h, y, first, dep):
         items = [(T["ps%d" % h][:, 0:32], T.ES[:, 15 - q:143 - q], T[y][:, q::16], first and q == 0, (not first) and q == 15) for q in range(16)]
         return mms(items, [dep])
 
-    def y1(h):
-        e = tt(T["ya%d" % h][:], T.V[:].indirect(T["ub%d" % h][:, 0:32]), T["r0%d" % h][:], A.is_equal, lb[h], mk[h][0], dV)
-        sums(h, "ya%d" % h, True, e)
+    def y1(h, first):
+        e = tt(T["ya%d" % h][:], T.V[:].indirect(T["uv%d" % h][:]), T["r0%d" % h][:], A.is_equal, lb[h], mk[h][0], dV)
+        return sums(h, "ya%d" % h, first, e)
 
-    def y2(h):
-        e = tt(T["yb%d" % h][:], T.W[:, 0:4097].indirect(T["ub%d" % h][:, 32:64]), T["r1%d" % h][:], A.max, lb[h], mk[h][1], dW)
-        res[h] = sums(h, "yb%d" % h, False, e)
+    def y2(h, first):
+        e = tt(T["yb%d" % h][:], T.W[:, 0:4097].indirect(T["ua%d" % h][:, 32:64]), T["r1%d" % h][:], A.max, lb[h], mk[h][1], dW)
+        return sums(h, "yb%d" % h, first, e)
 
-    def nxt(h, t):
+    def head(h, t):
         z = tt(T["z%d" % h][:], T["ps%d" % h][:, 0:32], T.cl[:, 32 * t:32 * t + 32], A.add, res[h])
-        ra, lb[h] = lists(h, z)
-        mk[h] = [mask0(h, ra), mask1(h, ra)]
+        ts(T["uv%d" % h][:], T["ps%d" % h][:, 0:32], 1.0 / 64, A.mult, -KC / 16.0 - 15.0 / 32, A.add)
+        mk[h][1] = mask1(h, rows(h, z))
+        pb[h] = parts(h)
 
-    y1(0)
-    y1(1)
-    y2(0)
-    y2(1)
-    nxt(0, 1)
+    def tail(h):
+        lb[h] = rest(h, pb[h])
+        mk[h][0] = mask0(h, lb[h])
+
+    y1(0, True)
+    res[0] = y2(0, False)
+    y2(1, True)
     for t in range(1, ST):
-        y1(0)
-        nxt(1, t)
-        y2(0)
-        y1(1)
-        if t + 1 < ST:
-            nxt(0, t + 1)
-        y2(1)
+        head(0, t)
+        res[1] = y1(1, False)
+        tail(0)
+        y2(0, True)
+        head(1, t)
+        res[0] = y1(0, False)
+        tail(1)
+        y2(1, True)
+    res[1] = y1(1, False)
     for h in range(2):
         e = ts(T["yo%d" % h][:], T["ps%d" % h][:, 0:32], 0.25, A.mult, -float(KC), A.add, res[h])
         waits(syn, "sy", [e])
         syn.dma_start(T.y[:, 32 * h:32 * h + 32], T["yo%d" % h][:]).then_inc(S["yd%d" % h], 16)
     waits(syn, "sy", [("yd0", 16), ("yd1", 16)])
-    g.wait_ge(S.ls, 2 * ne)
+    g.wait_ge(S.ls, 3 * ne)

@@ -5,12 +5,14 @@ from concourse.mybir import AluOpType as A, ActivationFunctionType as F
 
 NR, ST = 4, 8
 KC = 30718 - 2048
+BIG = 12582912.0
 SCRATCH = {
     "Xb": ("sbuf", [128, 4096], "bfloat16"), "Xe": ("sbuf", [128, 4096], "bfloat16"),
     "V": ("sbuf", [128, 16392], "int32"), "W": ("sbuf", [128, 4104], "float32"),
     "wi": ("sbuf", [128, 2048], "int32"),
-    "hi": ("sbuf", [128, 256], "int32"), "ni": ("sbuf", [128, 768], "int32"), "nf": ("sbuf", [128, 768], "float32"),
-    "zz": ("sbuf", [128, 256], "float32"), "kt": ("sbuf", [128, 256], "float16"),
+    "q0": ("sbuf", [128, 256], "float32"), "q1": ("sbuf", [128, 256], "float32"), "q2": ("sbuf", [128, 256], "float32"),
+    "e0": ("sbuf", [128, 256], "float32"), "e1": ("sbuf", [128, 256], "float32"), "e2": ("sbuf", [128, 256], "float32"),
+    "zz": ("sbuf", [128, 16], "float32"), "kt": ("sbuf", [128, 256], "float16"),
     "rt": ("sbuf", [128, 16], "float32"), "inc": ("sbuf", [128, 16], "float32"), "exc": ("sbuf", [128, 16], "float32"),
     "tq": ("sbuf", [128, 8], "float32"),
     "bs": ("sbuf", [128, 264], "float32"),
@@ -31,16 +33,17 @@ SCRATCH = {
 }
 for _k in range(NR):
     SCRATCH["wl%d" % _k] = ("sbuf", [128, 772], "float16")
-    for _h in range(2):
-        SCRATCH["vl%d%d" % (_k, _h)] = ("sbuf", [128, 256], "uint16")
+    SCRATCH["to%d" % _k] = ("sbuf", [128, 4], "float32")
+    SCRATCH["vl%d" % _k] = ("sbuf", [128, 512], "uint16")
 for _k in range(6):
     SCRATCH["dm%d" % _k] = ("sbuf", [128, 128], "float16")
 for _h in range(2):
     SCRATCH["ps%d" % _h] = ("psum", [128, 512], "float32")
     SCRATCH["z%d" % _h] = ("sbuf", [128, 32], "int32")
-    SCRATCH["la%d" % _h] = ("sbuf", [128, 64], "int32")
+    SCRATCH["la%d" % _h] = ("sbuf", [128, 32], "int32")
     SCRATCH["lb%d" % _h] = ("sbuf", [128, 64], "int32")
-    SCRATCH["ua%d" % _h] = ("sbuf", [128, 64], "uint16")
+    SCRATCH["ua%d" % _h] = ("sbuf", [128, 32], "uint16")
+    SCRATCH["ub%d" % _h] = ("sbuf", [128, 32], "uint16")
     SCRATCH["um%d" % _h] = ("sbuf", [128, 32], "uint16")
     SCRATCH["uv%d" % _h] = ("sbuf", [128, 32], "uint16")
     SCRATCH["r0%d" % _h] = ("sbuf", [128, 512], "bfloat16")
@@ -48,7 +51,7 @@ for _h in range(2):
     SCRATCH["ya%d" % _h] = ("sbuf", [128, 512], "float16")
     SCRATCH["yb%d" % _h] = ("sbuf", [128, 512], "float16")
     SCRATCH["yo%d" % _h] = ("sbuf", [128, 32], "float32")
-SEMAPHORES = ["sv", "sa", "st", "sg", "ls", "gx0", "gx1", "ldp", "yd0", "yd1"] + ["w%d" % k for k in range(NR)] + ["v%d%d" % (k, h) for k in range(NR) for h in range(2)]
+SEMAPHORES = ["sv", "sa", "st", "sg", "ls", "gx0", "gx1", "ldp", "yd0", "yd1"] + ["%s%d" % (s, k) for s in "wt" for k in range(NR)] + ["v%d%d" % (k, h) for k in range(NR) for h in range(2)]
 
 
 def rank_program(g, core, T, topo):
@@ -87,6 +90,9 @@ def rank_program(g, core, T, topo):
     def fill(ap, v, *deps):
         return op(vec, "sv", vec.memset, (ap, v), deps)
 
+    def scan(out, a, b, i, *deps):
+        return op(vec, "sv", vec.tensor_tensor_scan, (out, a, b, i, A.add, A.add), deps)
+
     def activ(out, in_, f, deps, **kw):
         return op(act, "sa", act.activation, (out, in_, f), deps, kw)
 
@@ -123,25 +129,30 @@ def rank_program(g, core, T, topo):
     b = ts(k1(tc, 6), k1(pf, 2), 2.0, A.mult, k1(tc, 4), A.add, b)
     dE = ts(T.E[:], T.xf[:], k1(tc, 3), A.is_equal, T.w4[:], A.mult, b, dx, dw)
     dP = ts(T.Pm[:], T.xf[:, 0:128], k1(tc, 6), A.is_equal, None, None, b)
-    fill(T.zz[:], 0.0)
-    fill(T.V[:, 16384:16392], 9)
-    fill(T.W[:, 4096:4104], -2048.0)
-    dS0 = ts(T["wl%d" % rank][:, 0:772:257], T.xi[:, 0:4], 0.0, A.mult, -2048.0, A.add)
+    mine = T["wl%d" % rank]
+
+    def constants_0():
+        fill(T.zz[:], 0.0)
+        fill(T.V[:, 16384:16392], 9)
+        fill(T.W[:, 4096:4104], -2048.0)
+        fill(T.e0[:], -BIG)
+        fill(T["to%d" % rank][:, 3:4], 0.0)
+        ts(mine[:, 0:772:257], T.xi[:, 0:4], 0.0, A.mult, -2048.0, A.add)
 
     def constants_1():
-        ts(T.Ih[:], T.xf[:, 0:128], k1(pf, 6), A.is_equal, None, None)
-        ts(T.In[:], T.xf[:, 0:128], k1(pf, 6), A.is_equal, -1.0, A.mult)
-        ts(T.kt[:], T.xi[:, 0:256], 16.0, A.mult, -8192.0, A.add)
-        ts(T.ES[:], T.xf[:], k1(tc, 5), A.is_equal, 4.0, A.mult)
         a = ts(T.xg[:], T.xi[:, 0:128], 112, A.bitwise_and, None, None)
-        ts(T.Lt[:], T.xf[:, 0:16], k1(pf, 4), A.is_gt, None, None)
+        c = ts(T.m0i[:, 0:64], T.xi[:, 0:64], 2, A.logical_shift_right, None, None)
+        d = ts(T.m0i[:, 64:128], T.xi[:, 0:64], 3, A.bitwise_and, None, None)
+        ts(T.Ih[:], T.xf[:, 0:128], k1(pf, 6), A.is_equal, None, None)
         ts(T.BO[:], T.xg[:], k1(pf, 5), A.is_equal, 1.0 / 2048, A.mult, a)
-        ts(T.m0i[:, 0:64], T.xi[:, 0:64], 2, A.logical_shift_right, None, None)
-        a = ts(T.m0i[:, 64:128], T.xi[:, 0:64], 3, A.bitwise_and, None, None)
-        ts(T.m0f[:, 0:64], T.m0i[:, 0:64], k1(pf, 4), A.is_gt, None, None, a)
-        a = ts(T.m0f[:, 64:128], T.m0i[:, 64:128], 1.0, A.add, None, None, a)
-        a = tt(T.m0f[:, 0:64], T.m0f[:, 0:64], T.m0f[:, 64:128], A.mult, a)
+        c = ts(T.m0f[:, 0:64], T.m0i[:, 0:64], k1(pf, 4), A.is_gt, None, None, c)
+        d = ts(T.m0f[:, 64:128], T.m0i[:, 64:128], 1.0, A.add, None, None, d)
+        ts(T.In[:], T.xf[:, 0:128], k1(pf, 6), A.is_equal, -1.0, A.mult)
+        a = tt(T.m0f[:, 0:64], T.m0f[:, 0:64], T.m0f[:, 64:128], A.mult, d)
+        ts(T.kt[:], T.xi[:, 0:256], 16.0, A.mult, -8192.0, A.add)
         ts(T.M0[:], T.m0f[:, 0:64], -1.0, A.add, None, None, a)
+        ts(T.ES[:], T.xf[:], k1(tc, 5), A.is_equal, 4.0, A.mult)
+        ts(T.Lt[:], T.xf[:, 0:16], k1(pf, 4), A.is_gt, None, None)
 
     def constants_2():
         a = ts(T.jq[:], T.xi[:], 15, A.bitwise_and, None, None)
@@ -170,11 +181,32 @@ def rank_program(g, core, T, topo):
 
     def constants_3():
         waits(vec, "sv", [("ldp", 32)])
-        ts(T.cl[:], T.pats_s[:], 1048577.0, A.mult, -4.0 * KC, A.add)
+        ts(T.st4[:], T.st_s[:], 4.0, A.mult, None, None)
+        d = ts(T.cz[:], T.pats_s[:, 0:32], 1048577.0, A.mult, None, None)
         for h in range(2):
             ts(T["uv%d" % h][:], T.st_s[:, 32 * h:32 * h + 32], 1.0 / 16, A.mult, -15.0 / 32, A.add)
-        ts(T.st4[:], T.st_s[:], 4.0, A.mult, None, None)
-        return ts(T.cz[:], T.pats_s[:, 0:32], 1048577.0, A.mult, None, None)
+        ts(T.cl[:], T.pats_s[:], 1048577.0, A.mult, -4.0 * KC, A.add)
+        return d
+
+    def rows(h, *deps):
+        return ts(T["um%d" % h][:], T["z%d" % h][:], 2.0 ** -14, A.mult, 2.0 ** -15 - 0.5, A.add, *deps)
+
+    def parts(h):
+        ts(T["lb%d" % h][:, 0:32], T["z%d" % h][:], 6, A.logical_shift_right, 255, A.bitwise_and)
+        return ts(T["lb%d" % h][:, 32:64], T["z%d" % h][:], 10, A.logical_shift_right, 0x1F00, A.bitwise_and)
+
+    def rest(h, b):
+        b = tt(T["ub%d" % h][:], T["lb%d" % h][:, 0:32], T["lb%d" % h][:, 32:64], A.add, b)
+        return b, ts(T["la%d" % h][:], T["z%d" % h][:], 63, A.bitwise_and, None, None)
+
+    def list0(h, l):
+        return activ(T["ua%d" % h][:], T["la%d" % h][:], F.Copy, [l])
+
+    def mask0(h, u):
+        return activ(T["r0%d" % h][:], T.M0[:].indirect(T["ua%d" % h][:]), F.Copy, [u])
+
+    def mask1(h, m, *deps):
+        return activ(T["r1%d" % h][:], T.M1[:, 0:257].indirect(T["um%d" % h][:]), F.Copy, [m] + list(deps))
 
     constants_1()
     dK = constants_3()
@@ -185,19 +217,25 @@ def rank_program(g, core, T, topo):
         pkd.append(mms([(T[bank][:, 0:256], T.E[sl, 15 - q:143 - q], T.Xb[sl, q:4096:16], q == 0, q == 15) for q in range(16)], [dE, ld[h]]))
     for j in range(4):
         sl = slice(1024 * j, 1024 * (j + 1))
-        e = activ(T.Xe[:, sl], T.Xb[:, sl], F.Exp, ld, scale=math.log(32.0))
+        e = activ(T.Xe[:, sl], T.Xb[:, sl], F.Exp, ld, scale=-math.log(64.0))
         hd = mms([(T.psh[:, 64 * j:64 * j + 64], T.Pm[:], T.Xe[:, 1024 * j + q:1024 * (j + 1):16], q == 0, q == 15) for q in range(16)], [dP, e])
+    dq = [activ(T["q%d" % c][:], T.psh[:, 0:256], F.Copy, [hd], scale=64.0 ** c, bias=BIG) for c in range(3)]
+    de = [None] + [activ(T["e%d" % c][:], T["q%d" % (c - 1)][:], F.Copy, [dq[c - 1]], scale=-64.0, bias=63 * BIG) for c in (1, 2)]
 
     ne = len(topo.engines(core, peers[0]))
 
-    def send(buf, sem, deps):
+    def send(ap, sem, deps):
         waits(g, "gq", deps)
         ids = [DstId(rid=topo.addr(p)[0], pnc=topo.addr(p)[1]) for p in peers]
-        g.remote_dma_fused([RemoteDMATransfer(dst_ids=ids, dma_engine_mask=topo.mask(core, peers[0]), remote_sem=S[sem], srcs=[T[buf][:]], dsts=[T[buf][:] for _ in peers])], local_sem=S.ls)
+        g.remote_dma_fused([RemoteDMATransfer(dst_ids=ids, dma_engine_mask=topo.mask(core, peers[0]), remote_sem=S[sem], srcs=[ap], dsts=[ap for _ in peers])], local_sem=S.ls)
 
     def unpack(r, h, k, dep):
         o = 4096 * r + 2048 * h + 256 * k
         ts(T.V[:, o:o + 256], T.wi[:, 512 * r + 256 * h:512 * r + 256 * h + 256], 2 * k, A.logical_shift_right, 3, A.bitwise_and, dep)
+
+    def top(r, h, *deps):
+        o = 4096 * r + 2048 * h + 256 * 7
+        return activ(T.V[:, o:o + 256], T["vl%d" % r][:, 256 * h:256 * h + 256], F.Copy, deps, scale=2.0 ** -14, bias=2.0 ** -15 - 0.5)
 
     def widen(r, banks, deps):
         def half(c):
@@ -212,135 +250,115 @@ def rank_program(g, core, T, topo):
             e = activ(T.W[:, 1024 * c + 256 * r:1024 * c + 256 * r + 256], T[banks[c // 2]][:, 256 * (c % 2):256 * (c % 2) + 256], F.Copy, [m])
         return e
 
-    def totals(r, *deps):
-        return ts(T.rt[:, r:12:4], T["wl%d" % r][:, 256:771:257], 2048.0, A.add, None, None, *deps)
-
-    def rows(h, *deps):
-        return ts(T["um%d" % h][:], T["z%d" % h][:], 2.0 ** -14, A.mult, 2.0 ** -15 - 0.5, A.add, *deps)
-
-    def parts(h):
-        ts(T["lb%d" % h][:, 0:32], T["z%d" % h][:], 6, A.logical_shift_right, 255, A.bitwise_and)
-        return ts(T["lb%d" % h][:, 32:64], T["z%d" % h][:], 10, A.logical_shift_right, 0x1F00, A.bitwise_and)
-
-    def rest(h, b):
-        la, lb = T["la%d" % h], T["lb%d" % h]
-        ts(la[:, 0:32], T["z%d" % h][:], 63, A.bitwise_and, None, None)
-        b = tt(la[:, 32:64], lb[:, 0:32], lb[:, 32:64], A.add, b)
-        return copy(T["ua%d" % h][:], la[:], b)
-
-    def mask0(h, u):
-        return activ(T["r0%d" % h][:], T.M0[:].indirect(T["ua%d" % h][:, 0:32]), F.Copy, [u])
-
-    def mask1(h, m, *deps):
-        return activ(T["r1%d" % h][:], T.M1[:, 0:257].indirect(T["um%d" % h][:]), F.Copy, [m] + list(deps))
-
-    constants_2()
-    own = []
-    for h, bank in enumerate(("psw", "pa")):
-        mine = "vl%d%d" % (rank, h)
-        cw = copy(T[mine][:], T[bank][:, 0:256], pkd[h])
-        send(mine, "v%d%d" % (rank, h), [cw])
-        own.append(copy(T.wi[:, 512 * rank + 256 * h:512 * rank + 256 * h + 256], T[bank][:, 0:256]))
-        for k in range(8):
-            unpack(rank, h, k, own[h])
     zr = [tt(T["z%d" % h][:], T.st4[:, 32 * h:32 * h + 32], T.cz[:], A.add, dK) for h in range(2)]
     um = [rows(h, zr[h]) for h in range(2)]
     pb = [parts(h) for h in range(2)]
     lb = [rest(h, pb[h]) for h in range(2)]
-    mk = [[mask0(h, lb[h]), None] for h in range(2)]
+    constants_0()
+    constants_2()
 
-    mine = "wl%d" % rank
-    dh = a = copy(T.hi[:], T.psh[:, 0:256], hd)
+    own, cw = [], []
+    for h, bank in enumerate(("psw", "pa")):
+        vl = T["vl%d" % rank][:, 256 * h:256 * h + 256]
+        cw.append(copy(vl, T[bank][:, 0:256], pkd[h]))
+        send(vl, "v%d%d" % (rank, h), [cw[h]])
+        own.append(copy(T.wi[:, 512 * rank + 256 * h:512 * rank + 256 * h + 256], T[bank][:, 0:256]))
+        for k in range(8 - h):
+            unpack(rank, h, k, own[h])
+
     for c in range(3):
-        b = ts(T.ni[:, 256 * c:256 * c + 256], T.hi[:], 5 * c, A.logical_shift_right, 31, A.bitwise_and, a)
-    b = copy(T.nf[:], T.ni[:], b)
-    for c in range(3):
-        s = op(vec, "sv", vec.tensor_tensor_scan, (T[mine][:, 257 * c + 1:257 * c + 257], T.nf[:, 256 * c:256 * c + 256], T.zz[:], -2048.0, A.add, A.add), (b, dS0))
-    send(mine, "w%d" % rank, [s])
-    one, two = ("psw", "psh"), ("pa", "pb")
-    store(rank, one, widen(rank, one, [s, own[0], own[1], dh]))
+        s = scan(mine[:, 257 * c + 1:257 * c + 257], T["q%d" % c][:], T["e%d" % c][:], -2048.0, *([dq[c], de[c]] if c else [dq[c]]))
+    a = to = ts(T["to%d" % rank][:, 0:3], mine[:, 256:771:257], 2048.0, A.add, None, None, s)
+    send(T["to%d" % rank][:], "t%d" % rank, [a])
+    send(mine[:], "w%d" % rank, [s])
 
     order = [(rank + NR - k) % NR for k in range(1, NR)]
-    last = order[2]
-    jobs = [(r, h, k) for h in range(2) for r in order for k in range(8)]
     at = {}
+    for r in order:
+        at[r] = activ(T.wi[:, 512 * r:512 * r + 512], T["vl%d" % r][:], F.Copy, [("v%d%d" % (r, h), ne) for h in range(2)])
+    top(rank, 1, cw[1])
+    u = [list0(h, lb[h][1]) for h in range(2)]
+    mk = [[mask0(h, u[h]), None] for h in range(2)]
+    one, two = ("psw", "psh"), ("pa", "pb")
+    free = store(rank, one, widen(rank, one, [s, own[0], own[1], de[2]]))
+    for h in range(2):
+        top(order[0], h, at[order[0]])
+
+    jobs = [(r, h, k) for r in order for h in range(2) for k in range(7)]
 
     def work(n):
         for r, h, k in jobs[:n]:
-            if k == 0:
-                at[r, h] = copy(T.wi[:, 512 * r + 256 * h:512 * r + 256 * h + 256], T["vl%d%d" % (r, h)][:], ("v%d%d" % (r, h), ne))
-            unpack(r, h, k, at[r, h])
+            unpack(r, h, k, at[r])
         del jobs[:n]
 
-    work(1)
-    totals(rank, s)
-    work(len(jobs) - 17)
-    free = ("sa", cnt["sa"])
-    w1 = widen(order[0], one, [("w%d" % order[0], ne), free])
-    w2 = widen(order[1], two, [("w%d" % order[1], ne)])
-    free = store(order[0], one, w1)
-    store(order[1], two, w2)
+    work(8)
+    copy(T.rt[:, rank:12:4], T["to%d" % rank][:, 0:3], to)
     for r in order:
-        dR = totals(r, ("w%d" % r, ne))
+        a = copy(T.rt[:, r:12:4], T["to%d" % r][:, 0:3], ("t%d" % r, ne))
     work(1)
-    a = tt(T.tq[:, 0:4], T.rt[:, 0:4], T.rt[:, 4:8], A.add, dR)
+    a = tt(T.tq[:, 0:4], T.rt[:, 0:4], T.rt[:, 4:8], A.add, a)
     work(1)
     a = tt(T.tq[:, 4:8], T.tq[:, 0:4], T.rt[:, 8:12], A.add, a)
     work(1)
     a = ts(T.rt[:, 12:16], T.tq[:, 4:8], -1.0, A.mult, 4096.0, A.add, a)
     work(1)
-    a = op(vec, "sv", vec.tensor_tensor_scan, (T.inc[:], T.rt[:], T.zz[:, 0:16], 131200.0, A.add, A.add), (a,))
+    a = scan(T.inc[:], T.rt[:], T.zz[:], 131200.0, a)
     work(1)
     b = copy(T.bs[:, 256:257], T.inc[:, 15:16], a)
     a = tt(T.exc[:], T.inc[:], T.rt[:], A.subtract, a)
-    work(1)
-    for k in range(9, 16):
+    for k in range(16):
         ba = activ(T.bs[:, 16 * k:16 * k + 16], T.Lt[:], F.Identity, [a], bias=k1(T.exc, k), scale=k1(T.rt, k))
-    for k in range(9):
-        b = ts(T.bs[:, 16 * k:16 * k + 16], T.Lt[:], k1(T.rt, k), A.mult, k1(T.exc, k), A.add, a)
     m = mms([(T.psm[:, 0:257], T.BO[:], T.bs[:, 0:257], True, True)], [b, ba])
-    w3 = widen(last, one, [("w%d" % last, ne), free])
-    dW = store(last, one, w3)
-    work(6)
+    for h in range(2):
+        top(order[1], h, at[order[1]])
     n = 257
-    a = ts(T.dh[:, 0:n], T.psm[:, 0:n], 1.0, A.mult, 2.0 ** -12 - 0.5, A.add, m)
-    work(1)
+    a = activ(T.dh[:, 0:n], T.psm[:, 0:n], F.Copy, [m], scale=1.0, bias=2.0 ** -12 - 0.5)
+    work(9)
     a = tt(T.dr[:, 0:n], T.psm[:, 0:n], T.dh[:, 0:n], A.subtract, a)
-    work(1)
-    a = ts(T.de[:, 0:n], T.dr[:, 0:n], 2048.0, A.mult, 2047.75, A.add, a)
+    for h in range(2):
+        dT = top(order[2], h, at[order[2]])
+    a = activ(T.de[:, 0:n], T.dr[:, 0:n], F.Copy, [a], scale=2048.0, bias=2047.75)
     for par in range(2):
         m = mms([(T.psd[:, par:par + 129] if par == 0 else T.psm[:, 0:128], T["dm%d" % (2 * i + par)][:], T[buf][:, par:257:2], i == 0, i == 2) for i, buf in enumerate(("dh", "de", "dr"))], [a])
-    work(len(jobs))
+    work(4)
     for par in range(2):
         n, end = 129 - par, 257 if par == 0 else 256
         dM = tt(T.M1[:, par:end:2], (T.psd if par == 0 else T.psm)[:, 0:n], T.km[:, par:end:2], A.add, m)
+    m0 = widen(order[0], two, [("w%d" % order[0], ne), own[1]])
+    m1 = widen(order[1], one, [("w%d" % order[1], ne), free])
+    free = store(order[0], two, m0)
+    store(order[1], one, m1)
     mk[0][1] = mask1(0, um[0], dM)
+    m2 = widen(order[2], two, [("w%d" % order[2], ne), free])
+    dW = store(order[2], two, m2)
     mk[1][1] = mask1(1, um[1], dM)
+    work(len(jobs))
     dV = ("sv", cnt["sv"])
 
-    res = [None, None]
+    res, du = [None, None], [dT, dT]
 
-    def sums(h, y, first, dep):
+    def sums(h, y, first, deps):
         items = [(T["ps%d" % h][:, 0:32], T.ES[:, 15 - q:143 - q], T[y][:, q::16], first and q == 0, (not first) and q == 15) for q in range(16)]
-        return mms(items, [dep])
+        return mms(items, deps)
 
     def y1(h, first):
-        e = tt(T["ya%d" % h][:], T.V[:].indirect(T["uv%d" % h][:]), T["r0%d" % h][:], A.is_equal, lb[h], mk[h][0], dV)
-        return sums(h, "ya%d" % h, first, e)
+        e = tt(T["ya%d" % h][:], T.V[:].indirect(T["uv%d" % h][:]), T["r0%d" % h][:], A.is_equal, du[h], mk[h][0], dV)
+        return sums(h, "ya%d" % h, first, [e])
 
     def y2(h, first):
-        e = tt(T["yb%d" % h][:], T.W[:, 0:4097].indirect(T["ua%d" % h][:, 32:64]), T["r1%d" % h][:], A.max, lb[h], mk[h][1], dW)
-        return sums(h, "yb%d" % h, first, e)
+        e = tt(T["yb%d" % h][:], T.W[:, 0:4097].indirect(T["ub%d" % h][:]), T["r1%d" % h][:], A.max, lb[h][0], mk[h][1], dW)
+        return sums(h, "yb%d" % h, first, [e, du[h]])
 
     def head(h, t):
         z = tt(T["z%d" % h][:], T["ps%d" % h][:, 0:32], T.cl[:, 32 * t:32 * t + 32], A.add, res[h])
-        ts(T["uv%d" % h][:], T["ps%d" % h][:, 0:32], 1.0 / 64, A.mult, -KC / 16.0 - 15.0 / 32, A.add)
         mk[h][1] = mask1(h, rows(h, z))
         pb[h] = parts(h)
 
     def tail(h):
         lb[h] = rest(h, pb[h])
-        mk[h][0] = mask0(h, lb[h])
+        u = list0(h, lb[h][1])
+        du[h] = activ(T["uv%d" % h][:], T["ps%d" % h][:, 0:32], F.Copy, [res[h]], scale=1.0 / 64, bias=-KC / 16.0 - 15.0 / 32)
+        mk[h][0] = mask0(h, u)
 
     y1(0, True)
     res[0] = y2(0, False)
@@ -360,4 +378,4 @@ def rank_program(g, core, T, topo):
         waits(syn, "sy", [e])
         syn.dma_start(T.y[:, 32 * h:32 * h + 32], T["yo%d" % h][:]).then_inc(S["yd%d" % h], 16)
     waits(syn, "sy", [("yd0", 16), ("yd1", 16)])
-    g.wait_ge(S.ls, 3 * ne)
+    g.wait_ge(S.ls, 4 * ne)

@@ -107,8 +107,8 @@ def rank_program(g, core, T, topo):
 
     def load(h):
         g.dma_start(T.Xb[64 * h:64 * h + 64, :], T.bwt[:, 32768 * h:32768 * h + 32768]).then_inc(S["gx%d" % h], 16)
-    load(0)
     g.iota(T.pi[:], [[1, 1]], 0, 1).then_inc(S.sg, 1)
+    load(0)
     g.iota(T.xi[:], [[1, 264]], 0, 0).then_inc(S.sg, 1)
     load(1)
     syn.dma_start(T.pats_s[:], T.pats[:]).then_inc(S.ldp, 16)
@@ -195,9 +195,11 @@ def rank_program(g, core, T, topo):
         ts(T["lb%d" % h][:, 0:32], T["z%d" % h][:], 6, A.logical_shift_right, 255, A.bitwise_and)
         return ts(T["lb%d" % h][:, 32:64], T["z%d" % h][:], 10, A.logical_shift_right, 0x1F00, A.bitwise_and)
 
-    def rest(h, b):
-        b = tt(T["ub%d" % h][:], T["lb%d" % h][:, 0:32], T["lb%d" % h][:, 32:64], A.add, b)
-        return b, ts(T["la%d" % h][:], T["z%d" % h][:], 63, A.bitwise_and, None, None)
+    def list_w(h, b):
+        return tt(T["ub%d" % h][:], T["lb%d" % h][:, 0:32], T["lb%d" % h][:, 32:64], A.add, b)
+
+    def list_q(h):
+        return ts(T["la%d" % h][:], T["z%d" % h][:], 63, A.bitwise_and, None, None)
 
     def list0(h, l):
         return activ(T["ua%d" % h][:], T["la%d" % h][:], F.Copy, [l])
@@ -211,16 +213,22 @@ def rank_program(g, core, T, topo):
     constants_1()
     dK = constants_3()
     ld = [("gx0", 16), ("gx1", 16)]
-    pkd = []
-    for h, bank in enumerate(("psw", "pa")):
+
+    def pack(h, bank):
         sl = slice(64 * h, 64 * h + 64)
-        pkd.append(mms([(T[bank][:, 0:256], T.E[sl, 15 - q:143 - q], T.Xb[sl, q:4096:16], q == 0, q == 15) for q in range(16)], [dE, ld[h]]))
+        return mms([(T[bank][:, 0:256], T.E[sl, 15 - q:143 - q], T.Xb[sl, q:4096:16], q == 0, q == 15) for q in range(16)], [dE, ld[h]])
+
+    pkd = [pack(0, "psw")]
     for j in range(4):
         sl = slice(1024 * j, 1024 * (j + 1))
         e = activ(T.Xe[:, sl], T.Xb[:, sl], F.Exp, ld, scale=-math.log(64.0))
         hd = mms([(T.psh[:, 64 * j:64 * j + 64], T.Pm[:], T.Xe[:, 1024 * j + q:1024 * (j + 1):16], q == 0, q == 15) for q in range(16)], [dP, e])
-    dq = [activ(T["q%d" % c][:], T.psh[:, 0:256], F.Copy, [hd], scale=64.0 ** c, bias=BIG) for c in range(3)]
-    de = [None] + [activ(T["e%d" % c][:], T["q%d" % (c - 1)][:], F.Copy, [dq[c - 1]], scale=-64.0, bias=63 * BIG) for c in (1, 2)]
+    pkd.append(pack(1, "pa"))
+    dq = []
+    for c in range(3):
+        dq.append(activ(T["q%d" % c][:], T.psh[:, 0:256], F.Copy, [hd], scale=64.0 ** c, bias=BIG))
+        if c < 2:
+            activ(T["e%d" % (c + 1)][:], T["q%d" % c][:], F.Copy, [dq[c]], scale=-64.0, bias=63 * BIG)
 
     ne = len(topo.engines(core, peers[0]))
 
@@ -229,69 +237,80 @@ def rank_program(g, core, T, topo):
         ids = [DstId(rid=topo.addr(p)[0], pnc=topo.addr(p)[1]) for p in peers]
         g.remote_dma_fused([RemoteDMATransfer(dst_ids=ids, dma_engine_mask=topo.mask(core, peers[0]), remote_sem=S[sem], srcs=[ap], dsts=[ap for _ in peers])], local_sem=S.ls)
 
-    def unpack(r, h, k, dep):
+    def words(b, r, h):
+        return T[b][:, 256 * h:256 * h + 256] if b != "wi" else T.wi[:, 512 * r + 256 * h:512 * r + 256 * h + 256]
+
+    def letter(r, h, k):
         o = 4096 * r + 2048 * h + 256 * k
-        ts(T.V[:, o:o + 256], T.wi[:, 512 * r + 256 * h:512 * r + 256 * h + 256], 2 * k, A.logical_shift_right, 3, A.bitwise_and, dep)
+        return T.V[:, o:o + 256]
+
+    def unpack(r, h, k, dep):
+        ts(letter(r, h, k), words("wi", r, h), 2 * k, A.logical_shift_right, 3, A.bitwise_and, dep)
 
     def top(r, h, *deps):
-        o = 4096 * r + 2048 * h + 256 * 7
-        return activ(T.V[:, o:o + 256], T["vl%d" % r][:, 256 * h:256 * h + 256], F.Copy, deps, scale=2.0 ** -14, bias=2.0 ** -15 - 0.5)
+        return activ(letter(r, h, 7), words("vl%d" % r, r, h), F.Copy, deps, scale=2.0 ** -14, bias=2.0 ** -15 - 0.5)
 
-    def widen(r, banks, deps):
-        def half(c):
-            return T[banks[c // 2]][:, 256 * (c % 2):256 * (c % 2) + 256]
+    def count(r, c):
+        return T["wl%d" % r][:, 257 * c:257 * c + 256]
 
-        def cnts(c):
-            return T["wl%d" % r][:, 257 * c:257 * c + 256]
-        return mms([(half(c), T.Ih[:], cnts(c), True, True) for c in range(3)] + [(half(3), T.Ih[:], T.kt[:], True, False)] + [(half(3), T.In[:], cnts(c), False, c == 2) for c in range(3)], deps)
+    def left(r, bank, deps):
+        return mms([(T[bank][:, 0:256], T.Ih[:], T.kt[:], True, False)] + [(T[bank][:, 0:256], T.In[:], count(r, c), False, c == 2) for c in range(3)], deps)
 
-    def store(r, banks, m):
+    def store(r, bank, m, *deps):
         for c in range(4):
-            e = activ(T.W[:, 1024 * c + 256 * r:1024 * c + 256 * r + 256], T[banks[c // 2]][:, 256 * (c % 2):256 * (c % 2) + 256], F.Copy, [m])
+            e = activ(T.W[:, 1024 * c + 256 * r:1024 * c + 256 * r + 256], count(r, c) if c < 3 else T[bank][:, 0:256], F.Copy, deps if c < 3 else [m])
         return e
 
     zr = [tt(T["z%d" % h][:], T.st4[:, 32 * h:32 * h + 32], T.cz[:], A.add, dK) for h in range(2)]
     um = [rows(h, zr[h]) for h in range(2)]
     pb = [parts(h) for h in range(2)]
-    lb = [rest(h, pb[h]) for h in range(2)]
+    la = [list_q(h) for h in range(2)]
+    lb = [list_w(h, pb[h]) for h in range(2)]
     constants_0()
     constants_2()
 
     own, cw = [], []
-    for h, bank in enumerate(("psw", "pa")):
-        vl = T["vl%d" % rank][:, 256 * h:256 * h + 256]
+
+    def letters(h, bank, n):
+        vl = words("vl%d" % rank, rank, h)
         cw.append(copy(vl, T[bank][:, 0:256], pkd[h]))
         send(vl, "v%d%d" % (rank, h), [cw[h]])
-        own.append(copy(T.wi[:, 512 * rank + 256 * h:512 * rank + 256 * h + 256], T[bank][:, 0:256]))
-        for k in range(8 - h):
+        own.append(copy(words("wi", rank, h), T[bank][:, 0:256]))
+        for k in range(n):
             unpack(rank, h, k, own[h])
 
-    for c in range(3):
-        s = scan(mine[:, 257 * c + 1:257 * c + 257], T["q%d" % c][:], T["e%d" % c][:], -2048.0, *([dq[c], de[c]] if c else [dq[c]]))
-    a = to = ts(T["to%d" % rank][:, 0:3], mine[:, 256:771:257], 2048.0, A.add, None, None, s)
-    send(T["to%d" % rank][:], "t%d" % rank, [a])
-    send(mine[:], "w%d" % rank, [s])
-
     order = [(rank + NR - k) % NR for k in range(1, NR)]
+    jobs = [(r, h, k) for h in range(2) for r in order for k in range(7)]
     at = {}
-    for r in order:
-        at[r] = activ(T.wi[:, 512 * r:512 * r + 512], T["vl%d" % r][:], F.Copy, [("v%d%d" % (r, h), ne) for h in range(2)])
-    top(rank, 1, cw[1])
-    u = [list0(h, lb[h][1]) for h in range(2)]
-    mk = [[mask0(h, u[h]), None] for h in range(2)]
-    one, two = ("psw", "psh"), ("pa", "pb")
-    free = store(rank, one, widen(rank, one, [s, own[0], own[1], de[2]]))
-    for h in range(2):
-        top(order[0], h, at[order[0]])
-
-    jobs = [(r, h, k) for r in order for h in range(2) for k in range(7)]
 
     def work(n):
         for r, h, k in jobs[:n]:
-            unpack(r, h, k, at[r])
+            unpack(r, h, k, at[r, h])
         del jobs[:n]
 
-    work(8)
+    def landed(r, h):
+        at[r, h] = activ(words("wi", r, h), words("vl%d" % r, r, h), F.Copy, [("v%d%d" % (r, h), ne)])
+
+    letters(0, "psw", 8)
+    for c in range(3):
+        s = scan(mine[:, 257 * c + 1:257 * c + 257], T["q%d" % c][:], T["e%d" % c][:], -2048.0, dq[c])
+    to = ts(T["to%d" % rank][:, 0:3], mine[:, 256:771:257], 2048.0, A.add, None, None, s)
+    send(T["to%d" % rank][:], "t%d" % rank, [to])
+    u = [list0(h, la[h]) for h in range(2)]
+    mk = [[mask0(h, u[h]), None] for h in range(2)]
+    landed(order[0], 0)
+    letters(1, "pa", 7)
+    send(mine[:], "w%d" % rank, [s])
+
+    landed(order[1], 0)
+    landed(order[2], 0)
+    top(rank, 1, cw[1])
+    m0 = left(rank, "psw", [s, own[0]])
+    store(rank, "psw", m0, s)
+    for r in order:
+        top(r, 0, at[r, 0])
+
+    work(6)
     copy(T.rt[:, rank:12:4], T["to%d" % rank][:, 0:3], to)
     for r in order:
         a = copy(T.rt[:, r:12:4], T["to%d" % r][:, 0:3], ("t%d" % r, ne))
@@ -309,14 +328,12 @@ def rank_program(g, core, T, topo):
     for k in range(16):
         ba = activ(T.bs[:, 16 * k:16 * k + 16], T.Lt[:], F.Identity, [a], bias=k1(T.exc, k), scale=k1(T.rt, k))
     m = mms([(T.psm[:, 0:257], T.BO[:], T.bs[:, 0:257], True, True)], [b, ba])
-    for h in range(2):
-        top(order[1], h, at[order[1]])
+    landed(order[0], 1)
     n = 257
     a = activ(T.dh[:, 0:n], T.psm[:, 0:n], F.Copy, [m], scale=1.0, bias=2.0 ** -12 - 0.5)
-    work(9)
+    work(12)
     a = tt(T.dr[:, 0:n], T.psm[:, 0:n], T.dh[:, 0:n], A.subtract, a)
-    for h in range(2):
-        dT = top(order[2], h, at[order[2]])
+    landed(order[1], 1)
     a = activ(T.de[:, 0:n], T.dr[:, 0:n], F.Copy, [a], scale=2048.0, bias=2047.75)
     for par in range(2):
         m = mms([(T.psd[:, par:par + 129] if par == 0 else T.psm[:, 0:128], T["dm%d" % (2 * i + par)][:], T[buf][:, par:257:2], i == 0, i == 2) for i, buf in enumerate(("dh", "de", "dr"))], [a])
@@ -324,13 +341,14 @@ def rank_program(g, core, T, topo):
     for par in range(2):
         n, end = 129 - par, 257 if par == 0 else 256
         dM = tt(T.M1[:, par:end:2], (T.psd if par == 0 else T.psm)[:, 0:n], T.km[:, par:end:2], A.add, m)
-    m0 = widen(order[0], two, [("w%d" % order[0], ne), own[1]])
-    m1 = widen(order[1], one, [("w%d" % order[1], ne), free])
-    free = store(order[0], two, m0)
-    store(order[1], one, m1)
-    mk[0][1] = mask1(0, um[0], dM)
-    m2 = widen(order[2], two, [("w%d" % order[2], ne), free])
-    dW = store(order[2], two, m2)
+    landed(order[2], 1)
+    banks = ("psh", "pa", "pb")
+    lf = [left(r, b, [("w%d" % r, ne), own[1], dq[2]]) for r, b in zip(order, banks)]
+    for i, r in enumerate(order):
+        dT = top(r, 1, at[r, 1])
+        if i == 2:
+            mk[0][1] = mask1(0, um[0], dM)
+        dW = store(r, banks[i], lf[i], ("w%d" % r, ne))
     mk[1][1] = mask1(1, um[1], dM)
     work(len(jobs))
     dV = ("sv", cnt["sv"])
@@ -346,19 +364,18 @@ def rank_program(g, core, T, topo):
         return sums(h, "ya%d" % h, first, [e])
 
     def y2(h, first):
-        e = tt(T["yb%d" % h][:], T.W[:, 0:4097].indirect(T["ub%d" % h][:]), T["r1%d" % h][:], A.max, lb[h][0], mk[h][1], dW)
+        e = tt(T["yb%d" % h][:], T.W[:, 0:4097].indirect(T["ub%d" % h][:]), T["r1%d" % h][:], A.max, lb[h], mk[h][1], dW)
         return sums(h, "yb%d" % h, first, [e, du[h]])
 
     def head(h, t):
         z = tt(T["z%d" % h][:], T["ps%d" % h][:, 0:32], T.cl[:, 32 * t:32 * t + 32], A.add, res[h])
         mk[h][1] = mask1(h, rows(h, z))
-        pb[h] = parts(h)
-
-    def tail(h):
-        lb[h] = rest(h, pb[h])
-        u = list0(h, lb[h][1])
+        u = list0(h, list_q(h))
         du[h] = activ(T["uv%d" % h][:], T["ps%d" % h][:, 0:32], F.Copy, [res[h]], scale=1.0 / 64, bias=-KC / 16.0 - 15.0 / 32)
         mk[h][0] = mask0(h, u)
+
+    def tail(h):
+        lb[h] = list_w(h, parts(h))
 
     y1(0, True)
     res[0] = y2(0, False)

import math
import numpy as np
from concourse.bass import DstId, RemoteDMATransfer
from concourse.mybir import AluOpType as A, ActivationFunctionType as F

NR, ST = 4, 8
KC = 30718 - 2048
BIG = 12582912.0
SCRATCH = {
    "Xb": ("sbuf", [128, 4096], "bfloat16"), "Xe": ("sbuf", [128, 4096], "bfloat16"),
    "V": ("sbuf", [128, 16392], "int32"), "W": ("sbuf", [128, 4104], "float32"),
    "wi": ("sbuf", [128, 2048], "int32"),
    "q0": ("sbuf", [128, 256], "float32"), "q1": ("sbuf", [128, 256], "float32"), "q2": ("sbuf", [128, 256], "float32"),
    "e0": ("sbuf", [128, 256], "float32"), "e1": ("sbuf", [128, 256], "float32"), "e2": ("sbuf", [128, 256], "float32"),
    "zz": ("sbuf", [128, 16], "float32"), "kt": ("sbuf", [128, 256], "float16"),
    "rt": ("sbuf", [128, 16], "float32"), "inc": ("sbuf", [128, 16], "float32"), "exc": ("sbuf", [128, 16], "float32"),
    "tq": ("sbuf", [128, 8], "float32"),
    "bs": ("sbuf", [128, 264], "float32"),
    "dh": ("sbuf", [128, 264], "float16"), "dr": ("sbuf", [128, 264], "float16"), "de": ("sbuf", [128, 264], "float16"),
    "M1": ("sbuf", [128, 264], "float32"),
    "M0": ("sbuf", [128, 64], "bfloat16"), "km": ("sbuf", [128, 264], "float32"), "jq": ("sbuf", [128, 264], "int32"),
    "xi": ("sbuf", [128, 264], "int32"), "xf": ("sbuf", [128, 144], "float32"), "pi": ("sbuf", [128, 1], "int32"),
    "pk": ("sbuf", [128, 8], "int32"), "pf": ("sbuf", [128, 8], "float32"), "tc": ("sbuf", [128, 40], "float32"),
    "w4": ("sbuf", [128, 1], "float32"),
    "E": ("sbuf", [128, 144], "bfloat16"), "ES": ("sbuf", [128, 144], "float16"),
    "Pm": ("sbuf", [128, 128], "bfloat16"), "Ih": ("sbuf", [128, 128], "float16"), "In": ("sbuf", [128, 128], "float16"),
    "xg": ("sbuf", [128, 128], "int32"), "BO": ("sbuf", [128, 128], "float32"),
    "Lt": ("sbuf", [128, 16], "float32"), "m0i": ("sbuf", [128, 128], "int32"), "m0f": ("sbuf", [128, 128], "float32"),
    "pats_s": ("sbuf", [128, 256], "int32"), "st_s": ("sbuf", [128, 64], "int32"), "cl": ("sbuf", [128, 256], "float32"),
    "cz": ("sbuf", [128, 32], "int32"), "st4": ("sbuf", [128, 64], "int32"),
    "psw": ("psum", [128, 512], "float32"), "psh": ("psum", [128, 512], "float32"), "psm": ("psum", [128, 512], "float32"),
    "psd": ("psum", [128, 512], "float32"), "pa": ("psum", [128, 512], "float32"), "pb": ("psum", [128, 512], "float32"),
}
for _k in range(NR):
    SCRATCH["wl%d" % _k] = ("sbuf", [128, 772], "float16")
    SCRATCH["to%d" % _k] = ("sbuf", [128, 4], "float32")
    SCRATCH["vl%d" % _k] = ("sbuf", [128, 512], "uint16")
for _k in range(6):
    SCRATCH["dm%d" % _k] = ("sbuf", [128, 128], "float16")
for _h in range(2):
    SCRATCH["ps%d" % _h] = ("psum", [128, 512], "float32")
    SCRATCH["z%d" % _h] = ("sbuf", [128, 32], "int32")
    SCRATCH["la%d" % _h] = ("sbuf", [128, 32], "int32")
    SCRATCH["lb%d" % _h] = ("sbuf", [128, 64], "int32")
    SCRATCH["ua%d" % _h] = ("sbuf", [128, 32], "uint16")
    SCRATCH["ub%d" % _h] = ("sbuf", [128, 32], "uint16")
    SCRATCH["um%d" % _h] = ("sbuf", [128, 32], "uint16")
    SCRATCH["uv%d" % _h] = ("sbuf", [128, 32], "uint16")
    SCRATCH["r0%d" % _h] = ("sbuf", [128, 512], "bfloat16")
    SCRATCH["r1%d" % _h] = ("sbuf", [128, 512], "float32")
    SCRATCH["ya%d" % _h] = ("sbuf", [128, 512], "float16")
    SCRATCH["yb%d" % _h] = ("sbuf", [128, 512], "float16")
    SCRATCH["yo%d" % _h] = ("sbuf", [128, 32], "float32")
SEMAPHORES = ["sv", "sa", "st", "sg", "ls", "gx0", "gx1", "ldp", "yd0", "yd1"] + ["%s%d" % (s, k) for s in "wt" for k in range(NR)] + ["v%d%d" % (k, h) for k in range(NR) for h in range(2)]


def rank_program(g, core, T, topo):
    rank = T.rank_of(core)
    if rank is None:
        return
    peers = [T.cores[(rank + d) % NR] for d in range(1, NR)]
    S = T.sem
    cnt, seen = {"sv": 0, "sa": 0, "st": 0, "sg": 0}, {}

    def waits(q, name, deps):
        for s, n in deps:
            if seen.get((name, s), 0) < n:
                q.wait_ge(S[s], n)
                seen[(name, s)] = n

    def op(q, name, call, args, deps, kw=None):
        waits(q, name, deps)
        call(*args, **(kw or {})).then_inc(S[name], 1)
        cnt[name] += 1
        return (name, cnt[name])

    vec, act, ten, syn = g.vector, g.scalar, g.tensor, g.sync

    def copy(out, in_, *deps):
        return op(vec, "sv", vec.tensor_copy, (out, in_), deps)

    def tt(out, a, b, o, *deps):
        return op(vec, "sv", vec.tensor_tensor, (out, a, b, o), deps)

    def ts(out, a, s1, o1, s2, o2, *deps):
        if o2 is None:
            return op(vec, "sv", vec.tensor_scalar, (out, a, s1, None, o1), deps)
        return op(vec, "sv", vec.tensor_scalar, (out, a, s1, s2, o1, o2), deps)

    def fill(ap, v, *deps):
        return op(vec, "sv", vec.memset, (ap, v), deps)

    def scan(out, a, b, i, *deps):
        return op(vec, "sv", vec.tensor_tensor_scan, (out, a, b, i, A.add, A.add), deps)

    def activ(out, in_, f, deps, **kw):
        return op(act, "sa", act.activation, (out, in_, f), deps, kw)

    def mms(items, deps):
        waits(ten, "st", deps)
        for i, (out, l, r, a, b) in enumerate(items):
            m = ten.matmul(out, l, r, a, b)
            if i == len(items) - 1:
                m.then_inc(S.st, 1)
        cnt["st"] += 1
        return ("st", cnt["st"])

    def load(h):
        g.dma_start(T.Xb[64 * h:64 * h + 64, :], T.bwt[:, 32768 * h:32768 * h + 32768]).then_inc(S["gx%d" % h], 16)
    g.iota(T.pi[:], [[1, 1]], 0, 1).then_inc(S.sg, 1)
    load(0)
    g.iota(T.xi[:], [[1, 264]], 0, 0).then_inc(S.sg, 1)
    load(1)
    syn.dma_start(T.pats_s[:], T.pats[:]).then_inc(S.ldp, 16)
    syn.dma_start(T.st_s[:], T.starts[:]).then_inc(S.ldp, 16)

    pk, pf, tc = T.pk, T.pf, T.tc

    def k1(b, i):
        return b[:, i:i + 1]
    for i, (sh, mk) in enumerate([(0, 1), (0, 7), (0, 56), (3, 1), (0, 15), (0, 112), (0, 127), (0, 64)]):
        d = ts(k1(pk, i), T.pi[:], sh, A.logical_shift_right, mk, A.bitwise_and, ("sg", 1))
    dp = copy(pf[:, 0:8], pk[:, 0:8], d)
    dw = activ(T.w4[:], k1(pf, 1), F.Exp, [dp], scale=math.log(4.0))
    dx = copy(T.xf[:], T.xi[:, 0:144], ("sg", 2))
    ts(k1(tc, 3), k1(pf, 2), 2.0, A.mult, 15.0, A.add, dp)
    b = ts(k1(tc, 4), k1(pf, 7), 0.125, A.mult, k1(pf, 1), A.add)
    ts(k1(tc, 5), k1(pf, 5), 15.0, A.add, None, None)
    b = ts(k1(tc, 6), k1(pf, 2), 2.0, A.mult, k1(tc, 4), A.add, b)
    dE = ts(T.E[:], T.xf[:], k1(tc, 3), A.is_equal, T.w4[:], A.mult, b, dx, dw)
    dP = ts(T.Pm[:], T.xf[:, 0:128], k1(tc, 6), A.is_equal, None, None, b)
    mine = T["wl%d" % rank]

    def constants_0():
        fill(T.zz[:], 0.0)
        fill(T.V[:, 16384:16392], 9)
        fill(T.W[:, 4096:4104], -2048.0)
        fill(T.e0[:], -BIG)
        fill(T["to%d" % rank][:, 3:4], 0.0)
        ts(mine[:, 0:772:257], T.xi[:, 0:4], 0.0, A.mult, -2048.0, A.add)

    def constants_1():
        a = ts(T.xg[:], T.xi[:, 0:128], 112, A.bitwise_and, None, None)
        c = ts(T.m0i[:, 0:64], T.xi[:, 0:64], 2, A.logical_shift_right, None, None)
        d = ts(T.m0i[:, 64:128], T.xi[:, 0:64], 3, A.bitwise_and, None, None)
        ts(T.Ih[:], T.xf[:, 0:128], k1(pf, 6), A.is_equal, None, None)
        ts(T.BO[:], T.xg[:], k1(pf, 5), A.is_equal, 1.0 / 2048, A.mult, a)
        c = ts(T.m0f[:, 0:64], T.m0i[:, 0:64], k1(pf, 4), A.is_gt, None, None, c)
        d = ts(T.m0f[:, 64:128], T.m0i[:, 64:128], 1.0, A.add, None, None, d)
        ts(T.In[:], T.xf[:, 0:128], k1(pf, 6), A.is_equal, -1.0, A.mult)
        a = tt(T.m0f[:, 0:64], T.m0f[:, 0:64], T.m0f[:, 64:128], A.mult, d)
        ts(T.kt[:], T.xi[:, 0:256], 16.0, A.mult, -8192.0, A.add)
        ts(T.M0[:], T.m0f[:, 0:64], -1.0, A.add, None, None, a)
        ts(T.ES[:], T.xf[:], k1(tc, 5), A.is_equal, 4.0, A.mult)
        ts(T.Lt[:], T.xf[:, 0:16], k1(pf, 4), A.is_gt, None, None)

    def constants_2():
        a = ts(T.jq[:], T.xi[:], 15, A.bitwise_and, None, None)
        ts(k1(tc, 8), k1(pf, 3), -448.0, A.mult, 448.0, A.add)
        for i, v in enumerate([9, 8]):
            ts(k1(tc, 10 + i), k1(pf, 4), float(v), A.is_equal, 256.0, A.mult)
        for i, v in enumerate([11, 10, 13, 12]):
            a = ts(k1(tc, 12 + i), k1(pf, 4), float(v), A.is_equal, None, None)
        b = tt(k1(tc, 18), k1(tc, 8), k1(pf, 0), A.mult, a)
        ts(T.km[:], T.jq[:], k1(pf, 4), A.is_equal, -6144.0, A.mult)
        b = tt(k1(tc, 19), k1(tc, 8), k1(tc, 18), A.subtract, b)
        c = ts(tc[:, 22:24], tc[:, 12:14], -2048.0, A.mult, 2048.0, A.add)
        b = tt(tc[:, 20:22], tc[:, 18:20], tc[:, 10:12], A.add, b)
        d = ts(tc[:, 24:26], tc[:, 14:16], 2046.0, A.mult, None, None)
        e = tt(tc[:, 26:28], tc[:, 12:14], tc[:, 14:16], A.subtract)
        ts(tc[:, 28:30], tc[:, 14:16], 2048.0, A.mult, None, None)
        f = ts(tc[:, 30:32], tc[:, 20:22], -1025.0, A.mult, None, None, b)
        d = tt(tc[:, 22:24], tc[:, 22:24], tc[:, 24:26], A.add, c, d)
        for i, col in enumerate([20, 26, 28]):
            for par in range(2):
                b = ts(T["dm%d" % (2 * i + par)][:], T.xf[:, 0:128], k1(pf, 6), A.is_equal, k1(tc, col + par), A.mult, f)
        d = tt(tc[:, 32:34], tc[:, 22:24], tc[:, 30:32], A.add, d, f)
        for par in range(2):
            end = 257 if par == 0 else 256
            ts(T.km[:, par:end:2], T.km[:, par:end:2], k1(tc, 32 + par), A.add, None, None, d)

    def constants_3():
        waits(vec, "sv", [("ldp", 32)])
        ts(T.st4[:], T.st_s[:], 4.0, A.mult, None, None)
        d = ts(T.cz[:], T.pats_s[:, 0:32], 1048577.0, A.mult, None, None)
        for h in range(2):
            ts(T["uv%d" % h][:], T.st_s[:, 32 * h:32 * h + 32], 1.0 / 16, A.mult, -15.0 / 32, A.add)
        ts(T.cl[:], T.pats_s[:], 1048577.0, A.mult, -4.0 * KC, A.add)
        return d

    def rows(h, *deps):
        return ts(T["um%d" % h][:], T["z%d" % h][:], 2.0 ** -14, A.mult, 2.0 ** -15 - 0.5, A.add, *deps)

    def parts(h):
        ts(T["lb%d" % h][:, 0:32], T["z%d" % h][:], 6, A.logical_shift_right, 255, A.bitwise_and)
        return ts(T["lb%d" % h][:, 32:64], T["z%d" % h][:], 10, A.logical_shift_right, 0x1F00, A.bitwise_and)

    def list_w(h, b):
        return tt(T["ub%d" % h][:], T["lb%d" % h][:, 0:32], T["lb%d" % h][:, 32:64], A.add, b)

    def list_q(h):
        return ts(T["la%d" % h][:], T["z%d" % h][:], 63, A.bitwise_and, None, None)

    def list0(h, l):
        return activ(T["ua%d" % h][:], T["la%d" % h][:], F.Copy, [l])

    def mask0(h, u):
        return activ(T["r0%d" % h][:], T.M0[:].indirect(T["ua%d" % h][:]), F.Copy, [u])

    def mask1(h, m, *deps):
        return activ(T["r1%d" % h][:], T.M1[:, 0:257].indirect(T["um%d" % h][:]), F.Copy, [m] + list(deps))

    constants_1()
    dK = constants_3()
    ld = [("gx0", 16), ("gx1", 16)]

    def pack(h, bank):
        sl = slice(64 * h, 64 * h + 64)
        return mms([(T[bank][:, 0:256], T.E[sl, 15 - q:143 - q], T.Xb[sl, q:4096:16], q == 0, q == 15) for q in range(16)], [dE, ld[h]])

    pkd = [pack(0, "psw")]
    for j in range(4):
        sl = slice(1024 * j, 1024 * (j + 1))
        e = activ(T.Xe[:, sl], T.Xb[:, sl], F.Exp, ld, scale=-math.log(64.0))
        hd = mms([(T.psh[:, 64 * j:64 * j + 64], T.Pm[:], T.Xe[:, 1024 * j + q:1024 * (j + 1):16], q == 0, q == 15) for q in range(16)], [dP, e])
    pkd.append(pack(1, "pa"))
    dq = []
    for c in range(3):
        dq.append(activ(T["q%d" % c][:], T.psh[:, 0:256], F.Copy, [hd], scale=64.0 ** c, bias=BIG))
        if c < 2:
            activ(T["e%d" % (c + 1)][:], T["q%d" % c][:], F.Copy, [dq[c]], scale=-64.0, bias=63 * BIG)

    ne = len(topo.engines(core, peers[0]))

    def send(ap, sem, deps):
        waits(g, "gq", deps)
        ids = [DstId(rid=topo.addr(p)[0], pnc=topo.addr(p)[1]) for p in peers]
        g.remote_dma_fused([RemoteDMATransfer(dst_ids=ids, dma_engine_mask=topo.mask(core, peers[0]), remote_sem=S[sem], srcs=[ap], dsts=[ap for _ in peers])], local_sem=S.ls)

    def words(b, r, h):
        return T[b][:, 256 * h:256 * h + 256] if b != "wi" else T.wi[:, 512 * r + 256 * h:512 * r + 256 * h + 256]

    def letter(r, h, k):
        o = 4096 * r + 2048 * h + 256 * k
        return T.V[:, o:o + 256]

    def unpack(r, h, k, dep):
        ts(letter(r, h, k), words("wi", r, h), 2 * k, A.logical_shift_right, 3, A.bitwise_and, dep)

    def top(r, h, *deps):
        return activ(letter(r, h, 7), words("vl%d" % r, r, h), F.Copy, deps, scale=2.0 ** -14, bias=2.0 ** -15 - 0.5)

    def count(r, c):
        return T["wl%d" % r][:, 257 * c:257 * c + 256]

    def left(r, bank, deps):
        return mms([(T[bank][:, 0:256], T.Ih[:], T.kt[:], True, False)] + [(T[bank][:, 0:256], T.In[:], count(r, c), False, c == 2) for c in range(3)], deps)

    def store(r, bank, m, *deps):
        for c in range(4):
            e = activ(T.W[:, 1024 * c + 256 * r:1024 * c + 256 * r + 256], count(r, c) if c < 3 else T[bank][:, 0:256], F.Copy, deps if c < 3 else [m])
        return e

    zr = [tt(T["z%d" % h][:], T.st4[:, 32 * h:32 * h + 32], T.cz[:], A.add, dK) for h in range(2)]
    um = [rows(h, zr[h]) for h in range(2)]
    pb = [parts(h) for h in range(2)]
    la = [list_q(h) for h in range(2)]
    lb = [list_w(h, pb[h]) for h in range(2)]
    constants_0()
    constants_2()

    own, cw = [], []

    def letters(h, bank, n):
        vl = words("vl%d" % rank, rank, h)
        cw.append(copy(vl, T[bank][:, 0:256], pkd[h]))
        send(vl, "v%d%d" % (rank, h), [cw[h]])
        own.append(copy(words("wi", rank, h), T[bank][:, 0:256]))
        for k in range(n):
            unpack(rank, h, k, own[h])

    order = [(rank + NR - k) % NR for k in range(1, NR)]
    jobs = [(r, h, k) for h in range(2) for r in order for k in range(7)]
    at = {}

    def work(n):
        for r, h, k in jobs[:n]:
            unpack(r, h, k, at[r, h])
        del jobs[:n]

    def landed(r, h):
        at[r, h] = activ(words("wi", r, h), words("vl%d" % r, r, h), F.Copy, [("v%d%d" % (r, h), ne)])

    letters(0, "psw", 8)
    for c in range(3):
        s = scan(mine[:, 257 * c + 1:257 * c + 257], T["q%d" % c][:], T["e%d" % c][:], -2048.0, dq[c])
    to = ts(T["to%d" % rank][:, 0:3], mine[:, 256:771:257], 2048.0, A.add, None, None, s)
    send(T["to%d" % rank][:], "t%d" % rank, [to])
    u = [list0(h, la[h]) for h in range(2)]
    mk = [[mask0(h, u[h]), None] for h in range(2)]
    landed(order[0], 0)
    letters(1, "pa", 7)
    send(mine[:], "w%d" % rank, [s])

    landed(order[1], 0)
    landed(order[2], 0)
    top(rank, 1, cw[1])
    m0 = left(rank, "psw", [s, own[0]])
    store(rank, "psw", m0, s)
    for r in order:
        top(r, 0, at[r, 0])

    work(6)
    copy(T.rt[:, rank:12:4], T["to%d" % rank][:, 0:3], to)
    for r in order:
        a = copy(T.rt[:, r:12:4], T["to%d" % r][:, 0:3], ("t%d" % r, ne))
    work(1)
    a = tt(T.tq[:, 0:4], T.rt[:, 0:4], T.rt[:, 4:8], A.add, a)
    work(1)
    a = tt(T.tq[:, 4:8], T.tq[:, 0:4], T.rt[:, 8:12], A.add, a)
    work(1)
    a = ts(T.rt[:, 12:16], T.tq[:, 4:8], -1.0, A.mult, 4096.0, A.add, a)
    work(1)
    a = scan(T.inc[:], T.rt[:], T.zz[:], 131200.0, a)
    work(1)
    b = copy(T.bs[:, 256:257], T.inc[:, 15:16], a)
    a = tt(T.exc[:], T.inc[:], T.rt[:], A.subtract, a)
    for k in range(16):
        ba = activ(T.bs[:, 16 * k:16 * k + 16], T.Lt[:], F.Identity, [a], bias=k1(T.exc, k), scale=k1(T.rt, k))
    m = mms([(T.psm[:, 0:257], T.BO[:], T.bs[:, 0:257], True, True)], [b, ba])
    landed(order[0], 1)
    n = 257
    a = activ(T.dh[:, 0:n], T.psm[:, 0:n], F.Copy, [m], scale=1.0, bias=2.0 ** -12 - 0.5)
    work(12)
    a = tt(T.dr[:, 0:n], T.psm[:, 0:n], T.dh[:, 0:n], A.subtract, a)
    landed(order[1], 1)
    a = activ(T.de[:, 0:n], T.dr[:, 0:n], F.Copy, [a], scale=2048.0, bias=2047.75)
    for par in range(2):
        m = mms([(T.psd[:, par:par + 129] if par == 0 else T.psm[:, 0:128], T["dm%d" % (2 * i + par)][:], T[buf][:, par:257:2], i == 0, i == 2) for i, buf in enumerate(("dh", "de", "dr"))], [a])
    work(4)
    for par in range(2):
        n, end = 129 - par, 257 if par == 0 else 256
        dM = tt(T.M1[:, par:end:2], (T.psd if par == 0 else T.psm)[:, 0:n], T.km[:, par:end:2], A.add, m)
    landed(order[2], 1)
    banks = ("psh", "pa", "pb")
    lf = [left(r, b, [("w%d" % r, ne), own[1], dq[2]]) for r, b in zip(order, banks)]
    for i, r in enumerate(order):
        dT = top(r, 1, at[r, 1])
        if i == 2:
            mk[0][1] = mask1(0, um[0], dM)
        dW = store(r, banks[i], lf[i], ("w%d" % r, ne))
    mk[1][1] = mask1(1, um[1], dM)
    work(len(jobs))
    dV = ("sv", cnt["sv"])

    res, du = [None, None], [dT, dT]

    def sums(h, y, first, deps):
        items = [(T["ps%d" % h][:, 0:32], T.ES[:, 15 - q:143 - q], T[y][:, q::16], first and q == 0, (not first) and q == 15) for q in range(16)]
        return mms(items, deps)

    def y1(h, first):
        e = tt(T["ya%d" % h][:], T.V[:].indirect(T["uv%d" % h][:]), T["r0%d" % h][:], A.is_equal, du[h], mk[h][0], dV)
        return sums(h, "ya%d" % h, first, [e])

    def y2(h, first):
        e = tt(T["yb%d" % h][:], T.W[:, 0:4097].indirect(T["ub%d" % h][:]), T["r1%d" % h][:], A.max, lb[h], mk[h][1], dW)
        return sums(h, "yb%d" % h, first, [e, du[h]])

    def head(h, t):
        z = tt(T["z%d" % h][:], T["ps%d" % h][:, 0:32], T.cl[:, 32 * t:32 * t + 32], A.add, res[h])
        mk[h][1] = mask1(h, rows(h, z))
        u = list0(h, list_q(h))
        du[h] = activ(T["uv%d" % h][:], T["ps%d" % h][:, 0:32], F.Copy, [res[h]], scale=1.0 / 64, bias=-KC / 16.0 - 15.0 / 32)
        mk[h][0] = mask0(h, u)

    def tail(h):
        lb[h] = list_w(h, parts(h))

    y1(0, True)
    res[0] = y2(0, False)
    y2(1, True)
    for t in range(1, ST):
        head(0, t)
        res[1] = y1(1, False)
        tail(0)
        y2(0, True)
        head(1, t)
        res[0] = y1(0, False)
        tail(1)
        y2(1, True)
    res[1] = y1(1, False)
    for h in range(2):
        e = ts(T["yo%d" % h][:], T["ps%d" % h][:, 0:32], 0.25, A.mult, -float(KC), A.add, res[h])
        waits(syn, "sy", [e])
        syn.dma_start(T.y[:, 32 * h:32 * h + 32], T["yo%d" % h][:]).then_inc(S["yd%d" % h], 16)
    waits(syn, "sy", [("yd0", 16), ("yd1", 16)])
    g.wait_ge(S.ls, 4 * ne)
